import numpy as np, ml_dtypes
CORES = [3,11,19,27,35,43,51,59]
N = 8
import mx_ref
BF = ml_dtypes.bfloat16
def cols(t, e):
    v = np.concatenate([t.reshape(128, -1, 4), np.zeros((128, 1, 4), BF)], axis=1)
    return np.ascontiguousarray(v[:, e]).reshape(128, -1)
def cut(t, i, w=512):
    return t[:, w * i:w * i + w]
def tile(rs):
    return np.stack(rs, axis=2).reshape(128, -1).astype(BF)
def pick(q, e):
    c = np.concatenate([q[0].reshape(128, -1, 4), np.zeros((128, 1, 4), np.uint8)], axis=1); s = np.concatenate([q[1], np.ones((16, 1), np.uint8)], axis=1)
    return (np.ascontiguousarray(c[:, e].reshape(128, -1)), np.ascontiguousarray(s[:, e]))
def join(*qs):
    return (np.concatenate([q[0] for q in qs], axis=1), np.concatenate([q[1] for q in qs], axis=1))
def put(q, e, v):
    c, s = q[0].reshape(128, -1, 4).copy(), q[1].copy(); c[:, e] = v[0].reshape(128, -1, 4); s[:, e] = v[1]
    return (c.reshape(128, -1), s)
def pk(c, s):
    return (np.ascontiguousarray(c), mx_ref.live(s))
def emit(q):
    return q[0], q[1]
def decode(q):
    o = []
    for b in range(4):
        e = np.zeros((128, 128, 4), np.float32); e[np.arange(128), np.arange(128), b] = 1
        o.append(mx_ref.matmul(mx_ref.quantize(e.reshape(128, 512).astype(BF)), q))
    return np.stack(o, axis=2).reshape(128, -1)
def f(rng, *shape):
    return mx_ref.flush((rng.standard_normal(shape, dtype=np.float32) * np.exp2(rng.integers(-2, 3, shape[:-1] + (1,)))).astype(BF))
def wide(rng, *shape, cols=0):
    v = rng.standard_normal(shape, dtype=np.float32) * np.exp2(rng.integers(-12, 13, shape)).astype(np.float32)
    if cols: v *= np.repeat(np.exp2(rng.integers(-cols, cols + 1, shape[:-2] + (1, shape[-1] // 4))) * (rng.random(shape[:-2] + (1, shape[-1] // 4)) > 0.0625), 4, axis=-1).astype(np.float32)
    return mx_ref.flush(v.astype(BF))
T, A, KM, CAPP, FA = 128, 32, 48, 16, 2
def big(t):
    t = np.array(t)
    t[np.abs(t.astype(np.float32)) < np.float32(2.0 ** -16)] = 0
    return t
def plain(rng):
    x = np.concatenate([f(rng, N, 128, 4 * A), f(rng, N, 128, 4 * (T - A))], axis=2)
    return {"x": big(x), "w": f(rng, N, 128, 2048), "v": f(rng, N, 128, 512)}
def pull(rng, x, at, who, n=8, bare=False):
    x = np.array(x).reshape(N, 128, T, 4)
    x[:, :n * len(at)] = 0
    for i, (q, a) in enumerate(at):
        if bare: x[q, :, a] = 0
        x[q, n * i:n * i + n, a] = (32 * (1 + rng.random((n, 4)))).astype(np.float32).astype(BF)
        r, j = np.nonzero(who == i)
        x[r, n * i:n * i + n, j] = (8 * (1 + rng.random((len(r), n, 4)))).astype(np.float32).astype(BF)
    return x.reshape(N, 128, 4 * T)
def setup_inputs(rng):
    return plain(rng)
def setup_inputs_crowd(rng):
    d, who = plain(rng), np.full((N, T), -1)
    z, q = int(rng.integers(1, N)), rng.permutation(N)[:2]
    for r in range(N):
        e = A + rng.permutation(T - A)[:KM * 5 // 6 + FA]
        who[r, e] = 0
        who[r, e[:FA]] = 1
    who[z, A:] = rng.integers(0, 2, T - A)
    d["x"] = pull(rng, d["x"], [(int(q[i]), int(rng.integers(0, A))) for i in range(2)], who)
    return d
def setup_inputs_full(rng):
    d, who, o = plain(rng), np.full((N, T), -1), rng.permutation(N)
    g = FA * A // CAPP
    e = np.tile(rng.permutation(A), FA).reshape(g, CAPP)
    for i, s in enumerate(np.sort(o[1:g + 1])):
        who[s, A:A + CAPP] = rng.permutation(e[i])
        who[s, A + CAPP:A + CAPP + 4] = e[-1, -1]
    d["x"] = pull(rng, d["x"], [(int(o[0]), a) for a in range(A)], who, 2, True)
    return d
def setup_inputs_ties(rng):
    d = plain(rng)
    x = np.array(d["x"])
    part = np.arange(128) // 8
    m = rng.permutation(N * A) % (N * A // 4)
    k = cols(np.concatenate([x[q][:, :4 * A] for q in range(N)], axis=1), rng.permutation(N * A)[m])
    k = np.abs(k.astype(np.float32)) * np.repeat(np.where(part[:, None] == m % 16, 2.0 ** -8, 1.0), 4, axis=1)
    k = big(k.astype(np.float32).astype(BF))
    for r in range(N):
        g = rng.permutation(np.arange(T - A) // 7)
        u = cols(np.ascontiguousarray(x[r][:, 4 * A:]), g)
        if r == 0:
            on = part[:, None] == (m[0] + 1 + g % 15) % 16
            u = (-np.abs(u.astype(np.float32)) * np.repeat(on, 4, axis=1)).astype(BF)
        if r == 1:
            u = np.abs(u.astype(np.float32)).reshape(128, T - A, 4)
            o = np.append(0, 1 + rng.permutation(T - A - 1)[KM // 2:])
            u[:, o[::2]] = -0.0
            u[:, o[1::2]] = 0.0
            u = u.astype(BF).reshape(128, -1)
        x[r][:, 4 * A:] = u
        x[r][:, :4 * A] = cut(k, r, 4 * A)
    d["x"] = x
    return d
def setup_inputs_own(rng):
    d = plain(rng)
    x = np.array(d["x"])
    x[:, :, 2 * A:4 * A] = -x[:, :, :2 * A]
    x[(np.arange(128) // (128 // N))[None, :] != np.arange(N)[:, None]] = 0
    d["x"] = x
    return d
def setup_inputs_spread(rng):
    return {**plain(rng), "x": big(wide(rng, N, 128, 4 * T, cols=4))}
def check_inputs(d):
    b = []
    for k in ("x", "w", "v"):
        t = np.abs(d[k].astype(np.float32))
        if not (np.isfinite(t).all() and ((t == 0) | (t >= 2.0 ** -30) & (t <= 2.0 ** 30)).all()): b.append("a value of " + k)
    return b
def choose(x):
    k = np.concatenate([x[q][:, :4 * A] for q in range(N)], axis=1)
    k = [mx_ref.quantize(np.ascontiguousarray(cut(k, i))) for i in range(N * A // 128)]
    goal, took, have = np.full((N, T), -1), np.full((N, A, FA), -1), np.zeros((N, A), int)
    for s in range(N):
        u = mx_ref.quantize(np.ascontiguousarray(x[s][:, 4 * A:]))
        z = np.concatenate([mx_ref.matmul(t, u) for t in k]) + np.float32(0.0)
        best = np.argmax(z, axis=0)
        offers = np.sort(np.argsort(-z.max(axis=0), kind="stable")[:KM])
        stand = np.zeros(N, int)
        for j in offers:
            q, a = best[j] // A, best[j] % A
            if stand[q] == CAPP: continue
            stand[q] += 1
            if have[q, a] == FA: continue
            took[q, a, have[q, a]] = s * T + A + j
            have[q, a] += 1
            goal[s, A + j] = q * T + a
    return goal, took
def reference(x, w, v):
    goal, took = choose(x)
    c = [mx_ref.quantize(np.ascontiguousarray(x[r])) for r in range(N)]
    d = np.concatenate([decode(c[r]).reshape(128, T, 4) for r in range(N)], axis=1)
    h = []
    for q in range(N):
        m = d[:, q * T:q * T + A].copy()
        for t in range(FA):
            a = np.flatnonzero(took[q, :, t] >= 0)
            m[:, a] = m[:, a] + d[:, took[q, a, t]]
        new = mx_ref.quantize(np.ascontiguousarray((m * np.float32(0.5)).reshape(128, -1).astype(BF)))
        a = np.flatnonzero(took[q, :, 0] >= 0)
        k = put(c[q], a, pick(new, a))
        rs = [np.maximum(mx_ref.matmul(mx_ref.quantize(np.ascontiguousarray(cut(w[q], i))), k), np.float32(0.0)) * np.float32(0.0625) for i in range(4)]
        h.append(mx_ref.quantize(np.ascontiguousarray(tile(rs))))
    every = join(*h)
    oc, osc = np.zeros((N, 128, 4 * T), np.uint8), np.zeros((N, 16, T), np.uint8)
    mg, y = np.zeros((N, 1, T), np.float32), np.zeros((N, 128, T), np.float32)
    for s in range(N):
        g = pick(every, np.where(goal[s] >= 0, goal[s], s * T + np.arange(T)))
        oc[s], osc[s] = emit(g)
        mg[s, 0] = goal[s]
        y[s] = mx_ref.matmul(mx_ref.quantize(np.ascontiguousarray(v[s])), g)
    return {"oc": oc, "osc": osc, "mg": mg, "y": y}

@@ -1,0 +1,383 @@
+from concourse.bass import DstId, RemoteDMATransfer
+from concourse.mybir import dt, AluOpType, AxisListType, ActivationFunctionType
+
+F32, BF, U16, I32, MXC, U8 = "float32", "bfloat16", "uint16", "int32", "float8_e4m3fn_x4", "uint8"
+SCRATCH = {}
+
+
+def _buf(name, cols, dtype):
+    SCRATCH[name] = ("sbuf", [128, cols], dtype)
+
+
+def _mx(name, cols):
+    _buf(name, cols, MXC)
+    _buf(name + "s", cols, U8)
+
+
+for _n, _c in (("qx", 128), ("anc", 288), ("qtri", 128), ("qa2", 128), ("qe", 512), ("qz", 128), ("qb", 128), ("qa", 128),
+               ("qb2", 128), ("snd", 128), ("slots", 256), ("pk", 192), ("qw", 512), ("qv", 128), ("km", 128),
+               ("hq", 128), ("hw", 384), ("fo", 128)):
+    _mx(_n, _c)
+for _n, _c in (("xt", 512), ("wt", 2048), ("vt", 512), ("ct", 1024), ("et", 2048), ("zt", 512), ("bt", 512), ("att", 512),
+               ("b2t", 512), ("zz", 512), ("mt", 512), ("ht", 512), ("hot", 512), ("ones", 128), ("ident", 128), ("tri", 128),
+               ("pm1", 128), ("rs", 256), ("lx", 128), ("arow", 128), ("eq", 256), ("cc", 256), ("c2", 256), ("j12", 256),
+               ("aw", 192), ("at", 128), ("adm4", 8), ("land3", 64), ("ax", 256), ("ar", 272), ("aj", 256), ("ajt", 256)):
+    _buf(_n, _c, BF)
+for _n, _c in (("z32", 288), ("R", 288), ("mrow", 96), ("thr", 96), ("t1", 96), ("t2", 97), ("sc", 16), ("jr", 256), ("j7", 8),
+               ("ab", 8), ("ab1", 8), ("qoh", 8), ("zc", 8), ("qi", 8), ("qc", 8), ("ri", 8), ("qh", 8), ("crow", 32),
+               ("row8", 8), ("row16", 16), ("pf", 4), ("pc", 8), ("m8", 8), ("m16", 16), ("jw", 8), ("jn", 8), ("lst", 8),
+               ("landL", 32), ("F4", 4), ("dan", 128), ("tb", 128), ("gw", 16), ("n1", 4), ("n2", 4), ("n3", 4), ("tmp", 8),
+               ("fa", 8), ("jf", 8), ("f1", 8), ("f2", 8), ("mw", 8), ("mw2", 8), ("yo", 128)):
+    _buf(_n, _c, F32)
+for _n, _c in (("il", 2), ("off", 8), ("fs", 4), ("sof", 4), ("posD", 16), ("fin", 8)):
+    _buf(_n, _c, U16)
+_buf("pi", 1, I32)
+_buf("pin", 4, I32)
+for _i in range(8):
+    SCRATCH["ps%d" % _i] = ("psum", [128, 512], F32)
+SEMAPHORES = (["cV", "cA", "cP", "cG", "a1", "o1s", "l2", "c2r", "o2a", "o2b", "m3", "o3a", "h3", "o3b"]
+              + ["d%d" % _i for _i in range(12)])
+
+
+def rank_program(g, core, T, topo):
+    r = T.rank_of(core)
+    if r is None:
+        return
+    N, S = len(T.cores), T.sem
+    A, CAPP, KM = 32, 16, 48
+    OP, AF, X = AluOpType, ActivationFunctionType, AxisListType.X
+    V, AC, PE, SY = g.vector, g.scalar, g.tensor, g.sync
+    tiny = 1e-29
+
+    qs = {"V": V, "A": AC, "P": PE, "G": g, "S": SY}
+    count, known = {}, {q: {} for q in qs}
+    writer, readers = {}, {}
+
+    def before(q, rd, wr):
+        need = [writer[k] for k in rd if k in writer]
+        for k in list(wr) + [k for k in rd if k.startswith("ps")]:
+            if k in writer:
+                need.append(writer[k])
+            need += readers.get(k, [])
+        best = {}
+        for s, v, clk in need:
+            if known[q].get(s, 0) < v and best.get(s, (0,))[0] < v:
+                best[s] = (v, clk)
+        for s in list(best):
+            if not any(o != s and best[o][1].get(s, 0) >= best[s][0] for o in best):
+                qs[q].wait_ge(S[s], best[s][0])
+        for s, (v, clk) in best.items():
+            known[q][s] = max(known[q].get(s, 0), v)
+            for a, b in clk.items():
+                known[q][a] = max(known[q].get(a, 0), b)
+
+    def after(tok, rd, wr):
+        for k in wr:
+            writer[k] = tok
+            readers[k] = []
+        for k in rd:
+            readers.setdefault(k, []).append(tok)
+
+    def op(q, rd, wr, fn, *args, **kw):
+        rd, wr = rd.split(), wr.split()
+        before(q, rd, wr)
+        s = "c" + q
+        count[s] = count.get(s, 0) + 1
+        fn(*args, **kw).then_inc(S[s], 1)
+        after((s, count[s], dict(known[q])), rd, wr)
+
+    dn = [0]
+
+    def dma(q, rd, wr, out, in_):
+        rd, wr = rd.split(), wr.split()
+        before(q, rd, wr)
+        s = "d%d" % dn[0]
+        dn[0] += 1
+        count[s] = 16
+        qs[q].dma_start(out, in_).then_inc(S[s], 16)
+        after((s, 16, dict(known[q])), rd, wr)
+
+    def arrive(s, n, wr):
+        count[s] = n
+        after((s, n, {}), [], wr.split())
+
+    order = [r ^ c for c in range(N)]
+    others = [T.cores[q] for q in order[1:]]
+    dst = {c: DstId(rid=topo.addr(c)[0], pnc=topo.addr(c)[1]) for c in others}
+    allm = topo.mask(core, others[0])
+    for c in others:
+        allm &= topo.mask(core, c)
+    eng = [e for e in topo.engines(core, others[0]) if allm >> e & 1]
+    width = len(eng)
+
+    def to_all(rd, src, dstap, sem, loc):
+        before("G", rd.split(), [])
+        g.remote_dma_fused([RemoteDMATransfer(dst_ids=[dst[c] for c in others], dma_engine_mask=allm, remote_sem=S[sem],
+                                              srcs=[src], dsts=[dstap] * len(others))], local_sem=S[loc])
+        count[loc] = count.get(loc, 0) + width
+
+    def to_each(rd, src, dstap, sem, loc):
+        before("G", rd.split(), [])
+        g.remote_dma_fused([RemoteDMATransfer(dst_ids=[dst[others[c - 1]]], dma_engine_mask=1 << eng[c - 1],
+                                              remote_sem=S[sem], src=src(c), dst=dstap) for c in range(1, N)],
+                           local_sem=S[loc])
+        count[loc] = count.get(loc, 0) + N - 1
+
+    def ts(rd, wr, out, in0, s1, s2, *ops):
+        op("V", rd, wr, V.tensor_scalar, out, in0, s1, s2, *ops)
+
+    def tt(rd, wr, out, in0, in1, o):
+        op("V", rd, wr, V.tensor_tensor, out, in0, in1, o)
+
+    def cp(rd, wr, out, in_):
+        op("V", rd, wr, V.tensor_copy, out, in_)
+
+    def fill(rd, wr, out, c):
+        op("V", rd, wr, V.memset, out, c)
+
+    def act(rd, wr, out, in_, f, **kw):
+        op("A", rd, wr, AC.activation, out, in_, f, **kw)
+
+    def mm(bank, w, wv, x, n, rd):
+        op("P", rd, "ps%d" % bank, PE.matmul_mx, T["ps%d" % bank][:, 0:n], T[w][:, wv:wv + 128], T[w + "s"][:, wv:wv + 128],
+           T[x][:, 0:n], T[x + "s"][:, 0:n], True, True)
+
+    def quant(out, a, n, tile, rd, wr, at=0):
+        op("V", rd, wr, V.quantize_mx, T[out][:, a:a + n], T[out + "s"][:, a:a + n], T[tile][:, at:at + 4 * n])
+
+    def pick(out, a, b, win, w, lists, la, lb, rd, wr):
+        cp(rd, wr, T[out][:, a:b].bitcast(dt.uint32), T[win][:, 0:w].bitcast(dt.uint32).indirect(T[lists][:, la:lb]))
+        act(rd, wr + "s", T[out + "s"][:, a:b], T[win + "s"][:, 0:w].indirect(T[lists][:, la:lb]), AF.Copy)
+
+    def layer(i, tile, n, wr, rd=""):
+        src, out = T["ps%d" % i][:, 0:n], T[tile][:, i:4 * n:4]
+        if i % 2:
+            ts("ps%d " % i + rd, wr, out, src, 0.0, 0.0625, OP.max, OP.mult)
+        else:
+            act("ps%d " % i + rd, wr, out, src, AF.Relu, scale=0.0625)
+
+    kw = {"allow_small_or_imprecise_dtypes": True}
+    sg = [-1 if r >> b & 1 else 1 for b in (2, 1, 0)]
+    dma("S", "", "xt", T.xt[:], T.x[:])
+    op("G", "", "pi", g.iota, T.pi[:], [[0, 1]], 0, 1)
+    op("G", "", "pm1", g.iota, T.pm1[:], [[0, 8], [1, 16]], 1, 0, **kw)
+    op("G", "", "qi", g.iota, T.qi[:], [[4 * A * sg[0], 2], [2 * A * sg[1], 2], [A * sg[2], 2]], A * r, 0, **kw)
+    op("G", "", "ri", g.iota, T.ri[:], [[A, 8]], 0, 0, **kw)
+    op("G", "", "crow", g.iota, T.crow[:], [[1, 32]], 0, 0, **kw)
+    fill("", "z32", T.z32[:], 0.0)
+    ts("pi", "pin", T.pin[:, 0:1], T.pi[:], 15, None, OP.bitwise_and)
+    ts("pin", "il0", T.il[:, 0:1], T.pin[:, 0:1], 0, None, OP.add)
+    ts("pin", "il1", T.il[:, 1:2], T.pin[:, 0:1], 16, None, OP.add)
+    for k, c in (("ones", 1.0), ("zt", 0.0), ("att", 0.0), ("bt", 0.0), ("ct", 0.0)):
+        fill("", k, T[k][:], c)
+    op("G", "ones", "tri", g.affine_select, T.tri[:], T.ones[:], [[1, 128]], OP.is_ge, 0.0, 0, -1)
+
+    quant("qx", 0, 128, "xt", "xt", "qx")
+    to_all("qx", T.qx[:, 0:A].bitcast(dt.uint8), T.anc[:, A * r:A * r + A].bitcast(dt.uint8), "a1", "o1s")
+    to_all("qx", T.qxs[:, 0:A], T.ancs[:, A * r:A * r + A], "a1", "o1s")
+    arrive("a1", 2 * width * (N - 1), "anc")
+    for a, k in ((A * r, "own"), (N * A, "pad")):
+        pick("anc", a, a + A, "qx", 128, "il", 0, 2, "qx il0 il1", "anc" + k)
+    SY.wait_ge(S.o1s, 2 * width)
+    known["S"]["o1s"] = 2 * width
+    dma("S", "", "wt", T.wt[:], T.w[:])
+    dma("S", "", "vt", T.vt[:], T.v[:])
+
+    op("G", "ones", "ident", g.affine_select, T.ident[:], T.ones[:], [[1, 128]], OP.is_equal, 0.0, 0, -1)
+    op("G", "", "row8", g.iota, T.row8[:], [[1, 8]], 0, 0, **kw)
+    op("G", "", "row16", g.iota, T.row16[:], [[1, 8], [0, 2]], 0, 0, **kw)
+    ts("pi", "pin1", T.pin[:, 1:2], T.pi[:], 4, None, OP.arith_shift_right)
+    ts("pi", "pin2", T.pin[:, 2:3], T.pi[:], 31, None, OP.bitwise_and)
+    cp("pin", "pm", T.pf[:, 0:1], T.pin[:, 0:1])
+    cp("pin1", "ph16", T.pf[:, 1:2], T.pin[:, 1:2])
+    cp("pin2", "p31", T.pf[:, 2:3], T.pin[:, 2:3])
+    ts("crow p31", "thr0", T.thr[:, 0:32], T.crow[:], T.pf[:, 2:3], -tiny, OP.is_lt, OP.mult)
+    fill("", "thr1", T.thr[:, 32:96], 0.0)
+    fill("thr1", "thr2", T.thr[64:128, 64:96], -tiny)
+    fill("thr2", "thr3", T.thr[96:128, 32:64], -tiny)
+    fill("", "kk", T.t2[:, 96:97], 0.5 - KM)
+    fill("kk", "kk", T.t2[0:32, 96:97], 1000.0)
+    fill("", "mq0", T.mrow[0:32, 32:96], 0.0)
+    ts("qi", "qc", T.qc[:], T.qi[:], 0.5 * A - 0.5, None, OP.add)
+    ts("ri", "qh", T.qh[:], T.ri[:], -0.5, None, OP.add)
+    ts("ph16", "khi", T.pc[:, 0:1], T.pf[:, 1:2], 16.0, None, OP.mult)
+    ts("pm", "a0", T.pc[:, 1:2], T.pf[:, 0:1], 1.0, None, OP.add)
+    ts("pm", "a1c", T.pc[:, 2:3], T.pf[:, 0:1], 17.0, None, OP.add)
+    ts("p31", "hp", T.pc[:, 3:4], T.pf[:, 2:3], 15.5, float(r % 2), OP.is_gt, OP.is_equal)
+    act("tri ct", "ctri", T.ct[:, 0:512:4], T.tri[:], AF.Copy)
+    quant("qtri", 0, 128, "ct", "ctri ct", "qtri")
+    fill("", "et", T.et[:], 0.0)
+    for b in range(4):
+        act("ident et", "e%d" % b, T.et[:, 512 * b + b:512 * b + 512:4], T.ident[:], AF.Copy, scale=0.5)
+    act("z32", "zz", T.zz[:, 0:256], T.z32[:, 0:256], AF.Copy)
+    act("z32", "zzb", T.zz[:, 256:512], T.z32[:, 0:256], AF.Copy)
+    for k in ("b2t", "mt", "ht"):
+        act("zz zzb", k, T[k][:], T.zz[:], AF.Copy)
+    quant("qe", 0, 512, "et", "et e0 e1 e2 e3", "qe")
+    for b in range(4):
+        mm(4 + b, "qe", 128 * b, "qx", 128, "qe qx")
+        act("ps%d" % (4 + b), "dan%d" % b, T.dan[:, 32 * b:32 * b + 32], T["ps%d" % (4 + b)][:, 0:A], AF.Copy)
+
+    best, q2, y1, lo, hi, u, o1 = [T.sc[:, i:i + 1] for i in range(7)]
+    M = T.R[:, 255:256]
+    mm(0, "qx", 0, "anc", 288, "qx anc ancown ancowns ancpad ancpads")
+    op("V", "ps0 z32", "R", V.tensor_tensor_scan, T.R[:], T.ps0[:, 0:288], T.z32[:], -9.0e29, OP.max, OP.add)
+    act("R", "best jr", T.jr[:], T.R[:, 0:256], AF.Sign, bias=M, scale=-1.0, accum_out=best)
+    act("best qc", "ab", T.ab[:], T.qc[:], AF.Abs, bias=best, scale=-1.0)
+    act("ab", "ab1", T.ab1[:], T.ab[:], AF.Copy, scale=1.0 / 64)
+    act("best qh", "q2 j7", T.j7[:, 0:7], T.qh[:, 1:8], AF.Sign, bias=best, scale=-1.0, accum_out=q2)
+    act("q2 best", "y1", y1, q2, AF.Identity, bias=best, scale=-16.0)
+    op("V", "R", "m0", V.transpose, T.mrow[:, 0:32], T.R[:, 256:288])
+    for a in range(1, 4):
+        for k in (1, 2):
+            b = (a - 1 + k) % 3 + 1
+            cp("m0", "m%d%d" % (a, k), T.mrow[32 * a:32 * a + 32, 32 * k:32 * k + 32], T.mrow[32 * b:32 * b + 32, 0:32])
+    ts("R m0 mq0 m11 m12 m21 m22 m31 m32", "t1", T.t1[:], T.mrow[:], M, None, OP.subtract)
+    tt("t1 thr0 thr1 thr2 thr3", "t2", T.t2[:, 0:96], T.t1[:], T.thr[:], OP.is_gt)
+    ts("ab", "qoh", T.qoh[:], T.ab[:], 16.0, None, OP.is_lt)
+    ts("y1", "lo", lo, y1, -111.0, 16.0, OP.add, OP.min)
+    ts("y1", "hi", hi, y1, -127.0, 0.0, OP.add, OP.max)
+    op("V", "t2 kk", "u", V.tensor_reduce, u, T.t2[:], X, OP.add)
+    ts("ab1 u zt", "ztv", T.zt[:, 0:32:4], T.ab1[:], u, 0.25, OP.max, OP.is_lt)
+    quant("qz", 0, 128, "zt", "ztv zt", "qz")
+    mm(1, "qtri", 0, "qz", 128, "qtri qz")
+    for k, (c, sc, rd) in enumerate(((0, T.pf[:, 0:1], "pm"), (1, T.pc[:, 0:1], "khi"), (32, lo, "lo"), (33, hi, "hi"))):
+        act("qoh bt " + rd, "b%d" % k, T.bt[:, c:c // 32 * 32 + 32:4], T.qoh[:], AF.Copy, scale=sc)
+    quant("qb", 0, 128, "bt", "bt b0 b1 b2 b3", "qb")
+    tt("ps1 ztv", "zc", T.zc[:], T.ps1[:, 0:8], T.zt[:, 0:32:4], OP.mult)
+    op("V", "zc", "o1", V.tensor_reduce, o1, T.zc[:], X, OP.add)
+    for t in range(2):
+        ts("pm1 o1 att", "at%d" % t, T.att[:, t:512:4], T.pm1[:], o1, None, OP.is_equal)
+    quant("qa", 0, 128, "att", "att at0 at1", "qa")
+    mm(2, "qa", 0, "qb", 128, "qa qb")
+
+    cp("ps2", "off", T.off[:], T.ps2[:, 0:8])
+    act("ps2 hp", "lst", T.lst[:], T.ps2[:, 8:16], AF.Copy, scale=T.pc[:, 3:4])
+    to_each("lst", lambda c: T.lst[:, c:c + 1], T.landL[:, 4 * r:4 * r + 1], "l2", "o2a")
+    pick("snd", 0, 128, "qx", 128, "off", 0, 8, "qx off", "snd")
+    to_each("snd", lambda c: T.snd[:, CAPP * c:CAPP * c + CAPP].bitcast(dt.uint8),
+            T.slots[:, CAPP * r:CAPP * r + CAPP].bitcast(dt.uint8), "c2r", "o2b")
+    to_each("snds", lambda c: T.snds[:, CAPP * c:CAPP * c + CAPP], T.slotss[:, CAPP * r:CAPP * r + CAPP], "c2r", "o2b")
+    arrive("l2", N - 1, "landL")
+    arrive("c2r", 2 * (N - 1), "slots")
+    pick("slots", CAPP * r, CAPP * r + CAPP, "qx", 128, "off", 0, 1, "qx off", "slown")
+    act("lst", "lown", T.landL[:, 4 * r:4 * r + 1], T.lst[:, 0:1], AF.Copy)
+
+    fill("", "rs", T.rs[:], 1.0)
+    fill("rs", "rs", T.rs[:, 0:1], 0.0)
+    fill("rs", "rs", T.rs[:, 128:129], 0.0)
+    quant("slots", 128, 128, "zz", "zz zzb", "slz")
+    quant("pk", 64, 128, "zz", "zz zzb", "pkz")
+    fill("", "aw", T.aw[:], 0.0)
+    ts("row8 pm", "jw", T.jw[:], T.row8[:], 16.0, T.pf[:, 0:1], OP.mult, OP.add)
+    quant("qw", 0, 512, "wt", "wt", "qw")
+    fill("", "ar0", T.ar[:, 256:272], 0.0)
+    fill("", "fa", T.fa[:], 0.0)
+    for t in range(3):
+        ts("pm1 a0 ct", "ca%d" % t, T.ct[:, 512 + t:1024:4], T.pm1[:], T.pc[:, 1:2], None, OP.is_equal)
+    ts("row8 ph16", "m8", T.m8[:], T.row8[:], T.pf[:, 1:2], None, OP.is_equal)
+    ts("row16 ph16", "m16", T.m16[:], T.row16[:], T.pf[:, 1:2], None, OP.is_equal)
+    ts("jw", "jn", T.jn[:], T.jw[:], -1.0, 127.0, OP.mult, OP.add)
+    quant("qa2", 0, 128, "ct", "ct ca0 ca1 ca2", "qa2", at=512)
+    st2, st, pl, ph, q32, q128, mn, mgc = [T.sc[:, i:i + 1] for i in range(7, 15)]
+    ts("o1", "st2", st2, o1, CAPP + 0.5, None, OP.is_lt)
+    ts("o1 st2", "st", st, o1, 0.5, st2, OP.is_gt, OP.mult)
+    ts("o1 st", "pl", pl, o1, -1.0, st, OP.add, OP.mult)
+    ts("q2", "q32", q32, q2, 16.0, 112.0, OP.mult, OP.add)
+    ts("q2", "q128", q128, q2, 64.0, 448.0, OP.mult, OP.add)
+    ts("q32 st", "ph", ph, q32, 16.0 * (r % 2) - 256.0, st, OP.add, OP.mult)
+    ts("ph", "ph", ph, ph, 256.0, None, OP.add)
+    for k, (c, n, m, sc, rd) in enumerate(((0, 16, "m16", pl, "pl"), (1, 16, "m16", ph, "ph"), (64, 8, "m8", lo, "lo"),
+                                           (65, 8, "m8", hi, "hi"), (66, 8, "m8", q32, "q32"), (96, 8, "m8", lo, "lo"),
+                                           (97, 8, "m8", hi, "hi"), (98, 8, "m8", q128, "q128"))):
+        ts(m + " b2t " + rd, "w%d" % k, T.b2t[:, c:c // 32 * 32 + 4 * n:4], T[m][:], sc, None, OP.mult)
+    quant("qb2", 0, 128, "b2t", "b2t " + " ".join("w%d" % k for k in range(8)), "qb2")
+    mm(3, "qa2", 0, "qb2", 128, "qa2 qb2")
+    cp("ps3", "posD", T.posD[:], T.ps3[:, 0:16])
+    cp("ps3", "gw", T.gw[:], T.ps3[:, 16:32])
+    tt("gw jn", "tmp", T.tmp[:], T.gw[:, 0:8], T.jn[:], OP.add)
+
+    for c in range(4):
+        la, lb = T.landL[:, 8 * c:8 * c + 1], T.landL[:, 8 * c + 4:8 * c + 5]
+        if c < 2:
+            ts("landL lown zz", "lx%d" % c, T.lx[:, 32 * c:32 * c + 32], T.zz[:, 0:32], la, lb, OP.add, OP.add)
+        else:
+            act("landL lown ones", "lx%d" % c, T.lx[:, 32 * c:32 * c + 32], T.ones[:, 0:32], AF.Identity, bias=lb, scale=la)
+    op("V", "lx0 lx1 lx2 lx3", "arow", V.transpose, T.arow[:], T.lx[:])
+    ts("arow a0", "eq0", T.eq[:, 0:128], T.arow[:], T.pc[:, 1:2], None, OP.is_equal)
+    ts("arow a1c", "eq1", T.eq[:, 128:256], T.arow[:], T.pc[:, 2:3], None, OP.is_equal)
+    op("V", "rs eq0 eq1", "cc", V.tensor_tensor_scan, T.cc[:], T.rs[:], T.eq[:], 0.0, OP.mult, OP.add)
+    for h in range(2):
+        act("cc", "F%d j%d" % (h, h), T.j12[:, 128 * h:128 * h + 128], T.cc[:, 128 * h:128 * h + 128], AF.Relu, bias=1.0,
+            scale=-1.0, accum_out=T.F4[:, h:h + 1])
+    ts("cc", "c2", T.c2[:], T.cc[:], 1.5, None, OP.is_lt)
+    for h in range(2):
+        op("V", "c2", "F%d" % (2 + h), V.tensor_reduce, T.F4[:, 2 + h:3 + h], T.c2[:, 128 * h:128 * h + 128], X, OP.add)
+    cp("F0 F1 F2 F3", "fs", T.fs[:], T.F4[:])
+
+    pick("pk", 0, 64, "slots", 256, "fs", 0, 4, "slots slown slowns slz fs", "pk")
+    for b in range(4):
+        mm(4 + b, "qe", 128 * b, "pk", 128, "qe pk pks pkz")
+    ts("F0 F1 F2 F3", "n1", T.n1[:], T.F4[:], 127.5, None, OP.is_gt)
+    tt("n1 jw", "n2", T.n2[:], T.n1[:], T.jw[:, 0:4], OP.mult)
+    tt("n2 F0 F1 F2 F3", "n3", T.n3[:], T.n2[:], T.F4[:], OP.add)
+    cp("n3", "sof", T.sof[:], T.n3[:])
+    cp("sof ones aw", "aws", T.aw[:, 0:192].indirect(T.sof[:, 0:4]), T.ones[:, 0:64])
+    op("V", "aws", "at", V.transpose, T.at[:], T.aw[:, 0:128])
+    cp("at", "adm4", T.adm4[:, 0:4], T.at[:, 0:128:32])
+    to_all("adm4", T.adm4[:, 0:4], T.land3[:, 8 * r:8 * r + 4], "m3", "o3a")
+    for k in range(5):
+        if k < 4:
+            tt("ps%d dan%d" % (4 + k, k), "tb%d" % k, T.tb[:, 32 * k:32 * k + 32], T["ps%d" % (4 + k)][:, 0:A],
+               T.dan[:, 32 * k:32 * k + 32], OP.add)
+        if k:
+            b = k - 1
+            tt("ps%d tb%d mt" % (4 + b, b), "mt%d" % b, T.mt[:, b:4 * A:4], T["ps%d" % (4 + b)][:, A:2 * A],
+               T.tb[:, 32 * b:32 * b + 32], OP.add)
+    quant("km", 0, 128, "mt", "mt mt0 mt1 mt2 mt3", "km")
+    for i in range(4):
+        mm(i, "qw", 128 * i, "km", 128, "qw km")
+        layer(i, "ht", A, "ht%d" % i, "ht")
+    quant("hq", 0, 128, "ht", "ht ht0 ht1 ht2 ht3", "hq")
+
+    to_all("hq", T.hq[:, 0:A].bitcast(dt.uint8), T.hw[:, 128 + A * r:128 + A * r + A].bitcast(dt.uint8), "h3", "o3b")
+    to_all("hq", T.hqs[:, 0:A], T.hws[:, 128 + A * r:128 + A * r + A], "h3", "o3b")
+    arrive("m3", width * (N - 1), "land3")
+    arrive("h3", 2 * width * (N - 1), "hwr")
+    cp("at", "adown", T.land3[:, 8 * r:8 * r + 4], T.at[:, 0:128:32])
+    for i in range(4):
+        mm(i, "qw", 128 * i, "qx", 128, "qw qx")
+        layer(i, "hot", 128, "ho%d" % i)
+    quant("hw", 0, 128, "hot", "ho0 ho1 ho2 ho3", "hwo")
+    pick("hw", 128 + A * r, 128 + A * r + A, "hq", 128, "il", 0, 2, "hq il0 il1", "hwn")
+    quant("qv", 0, 128, "vt", "vt", "qv")
+    ts("fa F0 F1", "fav", T.fa[:, 0:2], T.F4[:, 0:2], 127.5, 128.0 + A * r, OP.is_lt, OP.mult)
+    tt("fa fav jw", "jf", T.jf[:], T.fa[:], T.jw[:], OP.add)
+    for q in range(N):
+        col = T.land3[:, 8 * q + r // 2:8 * q + r // 2 + 1]
+        if q % 2:
+            ts("land3 adown ones", "ax%d" % q, T.ax[:, 32 * q:32 * q + 32], T.ones[:, 0:32], 0.0, col, OP.mult, OP.add)
+        else:
+            act("land3 adown zz", "ax%d" % q, T.ax[:, 32 * q:32 * q + 32], T.zz[:, 0:32], AF.Identity, bias=col)
+    op("V", " ".join("ax%d" % q for q in range(N)), "ar", V.transpose, T.ar[:, 0:256], T.ax[:])
+    cp("ar ar0 posD", "aj", T.aj[:], T.ar[:, 0:272].indirect(T.posD[:, 0:16]))
+    op("V", "aj", "ajt", V.transpose, T.ajt[:], T.aj[:])
+    tt("ajt tmp", "f1", T.f1[:], T.ajt[:, 0:256:32], T.tmp[:], OP.mult)
+    tt("f1 jf", "f2", T.f2[:], T.f1[:], T.jf[:], OP.add)
+    cp("f2", "fin", T.fin[:], T.f2[:])
+    tt("ajt gw", "mw", T.mw[:], T.ajt[:, 0:256:32], T.gw[:, 8:16], OP.mult)
+    tt("mw m8", "mw2", T.mw2[:], T.mw[:], T.m8[:], OP.mult)
+    op("V", "mw2", "mn", V.tensor_reduce, mn, T.mw2[:], X, OP.add)
+    ts("mn", "mgc", mgc, mn, -1.0, None, OP.add)
+    dma("S", "mgc", "mgo", T.mg[:], mgc)
+
+    pick("fo", 0, 128, "hw", 384, "fin", 0, 8, "hwo hwr hwn hwns fin", "fo")
+    mm(4, "qv", 0, "fo", 128, "qv fo fos")
+    dma("S", "fo", "oco", T.oc[:], T.fo[:].bitcast(dt.uint8))
+    for k in range(4):
+        dma("A", "fos", "osco%d" % k, T.osc[4 * k:4 * k + 4, :], T.fos[32 * k:32 * k + 4, :])
+    cp("ps4", "yo", T.yo[:], T.ps4[:, 0:128])
+    dma("S", "yo", "yout", T.y[:], T.yo[:])
+    for s, v in count.items():
+        if known["S"].get(s, 0) < v:
+            SY.wait_ge(S[s], v)

@@ -14,20 +14,21 @@ def _mx(name, cols):
     _buf(name + "s", cols, U8)
 
 
-for _n, _c in (("qx", 128), ("anc", 288), ("qtri", 128), ("qa2", 128), ("qe", 512), ("qz", 128), ("qb", 128), ("qa", 128),
-               ("qb2", 128), ("snd", 128), ("slots", 256), ("pk", 192), ("qw", 512), ("qv", 128), ("km", 128),
+for _n, _c in (("qx", 128), ("qn", 128), ("anc", 288), ("qtri", 128), ("qa2", 128), ("qe", 512), ("qz", 128), ("qb", 128),
+               ("qa", 128), ("qb2", 128), ("snd", 128), ("slots", 256), ("pk", 192), ("qw", 512), ("qv", 128), ("km", 128),
                ("hq", 128), ("hw", 384), ("fo", 128)):
     _mx(_n, _c)
-for _n, _c in (("xt", 512), ("wt", 2048), ("vt", 512), ("ct", 1024), ("et", 2048), ("zt", 512), ("bt", 512), ("att", 512),
-               ("b2t", 512), ("zz", 512), ("mt", 512), ("ht", 512), ("hot", 512), ("ones", 128), ("ident", 128), ("tri", 128),
-               ("pm1", 128), ("rs", 256), ("lx", 128), ("arow", 128), ("eq", 256), ("cc", 256), ("c2", 256), ("j12", 256),
-               ("aw", 192), ("at", 128), ("adm4", 8), ("land3", 64), ("ax", 256), ("ar", 272), ("aj", 256), ("ajt", 256)):
+for _n, _c in (("xt", 512), ("xa", 512), ("wt", 2048), ("vt", 512), ("ct", 1024), ("et", 2048), ("zt", 512), ("bt", 512),
+               ("att", 512), ("b2t", 512), ("zz", 512), ("mt", 512), ("ht", 512), ("hot", 512), ("ones", 128), ("ident", 128),
+               ("tri", 128), ("pm1", 128), ("rs", 256), ("lx", 128), ("arow", 128), ("eq", 256), ("cc", 256), ("c2", 256),
+               ("j12", 256), ("aw", 192), ("at", 128), ("adm4", 8), ("land3", 64), ("ax", 256), ("ar", 272), ("aj", 256),
+               ("ajt", 256)):
     _buf(_n, _c, BF)
 for _n, _c in (("z32", 288), ("R", 288), ("mrow", 96), ("thr", 96), ("t1", 96), ("t2", 97), ("sc", 16), ("jr", 256), ("j7", 8),
                ("ab", 8), ("ab1", 8), ("qoh", 8), ("zc", 8), ("qi", 8), ("qc", 8), ("ri", 8), ("qh", 8), ("crow", 32),
                ("row8", 8), ("row16", 16), ("pf", 4), ("pc", 8), ("m8", 8), ("m16", 16), ("jw", 8), ("jn", 8), ("lst", 8),
-               ("landL", 32), ("F4", 4), ("dan", 128), ("tb", 128), ("gw", 16), ("n1", 4), ("n2", 4), ("n3", 4), ("tmp", 8),
-               ("fa", 8), ("jf", 8), ("f1", 8), ("f2", 8), ("mw", 8), ("mw2", 8), ("yo", 128)):
+               ("landL", 32), ("F4", 4), ("dan", 128), ("tb", 128), ("n1", 4), ("n2", 4), ("n3", 4), ("tmp", 8),
+               ("jf", 8), ("f1", 8), ("f2", 8), ("mw2", 8), ("yo", 128)):
     _buf(_n, _c, F32)
 for _n, _c in (("il", 2), ("off", 8), ("fs", 4), ("sof", 4), ("posD", 16), ("fin", 8)):
     _buf(_n, _c, U16)
@@ -138,6 +139,9 @@ def rank_program(g, core, T, topo):
     def act(rd, wr, out, in_, f, **kw):
         op("A", rd, wr, AC.activation, out, in_, f, **kw)
 
+    def iota(wr, out, pattern, base=0, mult=0):
+        op("G", "", wr, g.iota, out, pattern, base, mult, allow_small_or_imprecise_dtypes=True)
+
     def mm(bank, w, wv, x, n, rd):
         op("P", rd, "ps%d" % bank, PE.matmul_mx, T["ps%d" % bank][:, 0:n], T[w][:, wv:wv + 128], T[w + "s"][:, wv:wv + 128],
            T[x][:, 0:n], T[x + "s"][:, 0:n], True, True)
@@ -149,43 +153,55 @@ def rank_program(g, core, T, topo):
         cp(rd, wr, T[out][:, a:b].bitcast(dt.uint32), T[win][:, 0:w].bitcast(dt.uint32).indirect(T[lists][:, la:lb]))
         act(rd, wr + "s", T[out + "s"][:, a:b], T[win + "s"][:, 0:w].indirect(T[lists][:, la:lb]), AF.Copy)
 
-    def layer(i, tile, n, wr, rd=""):
+    def layer(i, tile, n, wr, rd, both):
         src, out = T["ps%d" % i][:, 0:n], T[tile][:, i:4 * n:4]
-        if i % 2:
+        if i % 2 and both:
             ts("ps%d " % i + rd, wr, out, src, 0.0, 0.0625, OP.max, OP.mult)
         else:
             act("ps%d " % i + rd, wr, out, src, AF.Relu, scale=0.0625)
 
-    kw = {"allow_small_or_imprecise_dtypes": True}
-    sg = [-1 if r >> b & 1 else 1 for b in (2, 1, 0)]
+    dma("S", "", "xa", T.xa[:, 0:4 * A], T.x[:, 0:4 * A])
     dma("S", "", "xt", T.xt[:], T.x[:])
+    sg = [-1 if r >> b & 1 else 1 for b in (2, 1, 0)]
     op("G", "", "pi", g.iota, T.pi[:], [[0, 1]], 0, 1)
-    op("G", "", "pm1", g.iota, T.pm1[:], [[0, 8], [1, 16]], 1, 0, **kw)
-    op("G", "", "qi", g.iota, T.qi[:], [[4 * A * sg[0], 2], [2 * A * sg[1], 2], [A * sg[2], 2]], A * r, 0, **kw)
-    op("G", "", "ri", g.iota, T.ri[:], [[A, 8]], 0, 0, **kw)
-    op("G", "", "crow", g.iota, T.crow[:], [[1, 32]], 0, 0, **kw)
+    iota("qi", T.qi[:], [[4 * A * sg[0], 2], [2 * A * sg[1], 2], [A * sg[2], 2]], A * r)
+    iota("ri", T.ri[:], [[A, 8]])
+    iota("crow", T.crow[:], [[1, 32]])
     fill("", "z32", T.z32[:], 0.0)
+    fill("", "ones", T.ones[:], 1.0)
+    fill("", "xaz", T.xa[:, 4 * A:], 0.0)
     ts("pi", "pin", T.pin[:, 0:1], T.pi[:], 15, None, OP.bitwise_and)
     ts("pin", "il0", T.il[:, 0:1], T.pin[:, 0:1], 0, None, OP.add)
     ts("pin", "il1", T.il[:, 1:2], T.pin[:, 0:1], 16, None, OP.add)
-    for k, c in (("ones", 1.0), ("zt", 0.0), ("att", 0.0), ("bt", 0.0), ("ct", 0.0)):
-        fill("", k, T[k][:], c)
     op("G", "ones", "tri", g.affine_select, T.tri[:], T.ones[:], [[1, 128]], OP.is_ge, 0.0, 0, -1)
+    for h in range(2):
+        act("z32", "zz%d" % h, T.zz[:, 256 * h:256 * h + 256], T.z32[:, 0:256], AF.Copy)
+    for k in ("mt", "ht"):
+        act("zz0 zz1", k, T[k][:], T.zz[:], AF.Copy)
+    for b in range(4):
+        act("zz0 zz1", "et%d" % b, T.et[:, 512 * b:512 * b + 512], T.zz[:], AF.Copy)
+    for k in ("zt", "att", "bt"):
+        fill("", k, T[k][:], 0.0)
 
-    quant("qx", 0, 128, "xt", "xt", "qx")
-    to_all("qx", T.qx[:, 0:A].bitcast(dt.uint8), T.anc[:, A * r:A * r + A].bitcast(dt.uint8), "a1", "o1s")
-    to_all("qx", T.qxs[:, 0:A], T.ancs[:, A * r:A * r + A], "a1", "o1s")
+    quant("qn", 0, 128, "xa", "xa xaz", "qn")
+    to_all("qn", T.qn[:, 0:A].bitcast(dt.uint8), T.anc[:, A * r:A * r + A].bitcast(dt.uint8), "a1", "o1s")
+    to_all("qn", T.qns[:, 0:A], T.ancs[:, A * r:A * r + A], "a1", "o1s")
     arrive("a1", 2 * width * (N - 1), "anc")
     for a, k in ((A * r, "own"), (N * A, "pad")):
-        pick("anc", a, a + A, "qx", 128, "il", 0, 2, "qx il0 il1", "anc" + k)
+        pick("anc", a, a + A, "qn", 128, "il", 0, 2, "qn il0 il1", "anc" + k)
+    quant("qx", 0, 128, "xt", "xt", "qx")
     SY.wait_ge(S.o1s, 2 * width)
     known["S"]["o1s"] = 2 * width
     dma("S", "", "wt", T.wt[:], T.w[:])
     dma("S", "", "vt", T.vt[:], T.v[:])
 
     op("G", "ones", "ident", g.affine_select, T.ident[:], T.ones[:], [[1, 128]], OP.is_equal, 0.0, 0, -1)
-    op("G", "", "row8", g.iota, T.row8[:], [[1, 8]], 0, 0, **kw)
-    op("G", "", "row16", g.iota, T.row16[:], [[1, 8], [0, 2]], 0, 0, **kw)
+    iota("pm1", T.pm1[:], [[0, 8], [1, 16]], 1)
+    iota("row8", T.row8[:], [[1, 8]])
+    iota("row16", T.row16[:], [[1, 8], [0, 2]])
+    iota("b2t", T.b2t[:], [[0, 512]])
+    fill("", "ct", T.ct[:], 0.0)
+    act("tri ct", "ctri", T.ct[:, 0:512:4], T.tri[:], AF.Copy)
     ts("pi", "pin1", T.pin[:, 1:2], T.pi[:], 4, None, OP.arith_shift_right)
     ts("pi", "pin2", T.pin[:, 2:3], T.pi[:], 31, None, OP.bitwise_and)
     cp("pin", "pm", T.pf[:, 0:1], T.pin[:, 0:1])
@@ -204,48 +220,55 @@ def rank_program(g, core, T, topo):
     ts("pm", "a0", T.pc[:, 1:2], T.pf[:, 0:1], 1.0, None, OP.add)
     ts("pm", "a1c", T.pc[:, 2:3], T.pf[:, 0:1], 17.0, None, OP.add)
     ts("p31", "hp", T.pc[:, 3:4], T.pf[:, 2:3], 15.5, float(r % 2), OP.is_gt, OP.is_equal)
-    act("tri ct", "ctri", T.ct[:, 0:512:4], T.tri[:], AF.Copy)
     quant("qtri", 0, 128, "ct", "ctri ct", "qtri")
-    fill("", "et", T.et[:], 0.0)
     for b in range(4):
-        act("ident et", "e%d" % b, T.et[:, 512 * b + b:512 * b + 512:4], T.ident[:], AF.Copy, scale=0.5)
-    act("z32", "zz", T.zz[:, 0:256], T.z32[:, 0:256], AF.Copy)
-    act("z32", "zzb", T.zz[:, 256:512], T.z32[:, 0:256], AF.Copy)
-    for k in ("b2t", "mt", "ht"):
-        act("zz zzb", k, T[k][:], T.zz[:], AF.Copy)
-    quant("qe", 0, 512, "et", "et e0 e1 e2 e3", "qe")
-    for b in range(4):
-        mm(4 + b, "qe", 128 * b, "qx", 128, "qe qx")
-        act("ps%d" % (4 + b), "dan%d" % b, T.dan[:, 32 * b:32 * b + 32], T["ps%d" % (4 + b)][:, 0:A], AF.Copy)
+        act("ident et%d" % b, "e%d" % b, T.et[:, 512 * b + b:512 * b + 512:4], T.ident[:], AF.Copy, scale=0.5)
+    fill("", "rs", T.rs[:], 1.0)
+    fill("rs", "rs", T.rs[:, 0:1], 0.0)
+    fill("rs", "rs", T.rs[:, 128:129], 0.0)
+    quant("slots", 128, 128, "zz", "zz0 zz1", "slz")
+    quant("pk", 64, 128, "zz", "zz0 zz1", "pkz")
+    fill("", "aw", T.aw[:], 0.0)
+    ts("row8 pm", "jw", T.jw[:], T.row8[:], 16.0, T.pf[:, 0:1], OP.mult, OP.add)
+    ts("jw", "jn", T.jn[:], T.jw[:], -1.0, 127.0, OP.mult, OP.add)
+    ts("row8 ph16", "m8", T.m8[:], T.row8[:], T.pf[:, 1:2], None, OP.is_equal)
+    ts("row16 ph16", "m16", T.m16[:], T.row16[:], T.pf[:, 1:2], None, OP.is_equal)
+    for t in range(3):
+        ts("pm1 a0 ct", "ca%d" % t, T.ct[:, 512 + t:1024:4], T.pm1[:], T.pc[:, 1:2], None, OP.is_equal)
+    quant("qa2", 0, 128, "ct", "ct ca0 ca1 ca2", "qa2", at=512)
 
-    best, q2, y1, lo, hi, u, o1 = [T.sc[:, i:i + 1] for i in range(7)]
+    best, q2, y1, lo, hi, u, o1, st2, st, pl, ph, q32, gn, mn, mgc = [T.sc[:, i:i + 1] for i in range(15)]
     M = T.R[:, 255:256]
     mm(0, "qx", 0, "anc", 288, "qx anc ancown ancowns ancpad ancpads")
     op("V", "ps0 z32", "R", V.tensor_tensor_scan, T.R[:], T.ps0[:, 0:288], T.z32[:], -9.0e29, OP.max, OP.add)
+    op("V", "R", "m0", V.transpose, T.mrow[:, 0:32], T.R[:, 256:288])
+    for a in range(1, 4):
+        for k in (1, 2):
+            b = (a - 1 + k) % 3 + 1
+            to, of = T.mrow[32 * a:32 * a + 32, 32 * k:32 * k + 32], T.mrow[32 * b:32 * b + 32, 0:32]
+            if k == 1:
+                cp("m0", "m%d%d" % (a, k), to, of)
+            else:
+                act("m0", "m%d%d" % (a, k), to, of, AF.Copy)
     act("R", "best jr", T.jr[:], T.R[:, 0:256], AF.Sign, bias=M, scale=-1.0, accum_out=best)
     act("best qc", "ab", T.ab[:], T.qc[:], AF.Abs, bias=best, scale=-1.0)
     act("ab", "ab1", T.ab1[:], T.ab[:], AF.Copy, scale=1.0 / 64)
     act("best qh", "q2 j7", T.j7[:, 0:7], T.qh[:, 1:8], AF.Sign, bias=best, scale=-1.0, accum_out=q2)
     act("q2 best", "y1", y1, q2, AF.Identity, bias=best, scale=-16.0)
-    op("V", "R", "m0", V.transpose, T.mrow[:, 0:32], T.R[:, 256:288])
-    for a in range(1, 4):
-        for k in (1, 2):
-            b = (a - 1 + k) % 3 + 1
-            cp("m0", "m%d%d" % (a, k), T.mrow[32 * a:32 * a + 32, 32 * k:32 * k + 32], T.mrow[32 * b:32 * b + 32, 0:32])
     ts("R m0 mq0 m11 m12 m21 m22 m31 m32", "t1", T.t1[:], T.mrow[:], M, None, OP.subtract)
     tt("t1 thr0 thr1 thr2 thr3", "t2", T.t2[:, 0:96], T.t1[:], T.thr[:], OP.is_gt)
-    ts("ab", "qoh", T.qoh[:], T.ab[:], 16.0, None, OP.is_lt)
-    ts("y1", "lo", lo, y1, -111.0, 16.0, OP.add, OP.min)
-    ts("y1", "hi", hi, y1, -127.0, 0.0, OP.add, OP.max)
     op("V", "t2 kk", "u", V.tensor_reduce, u, T.t2[:], X, OP.add)
     ts("ab1 u zt", "ztv", T.zt[:, 0:32:4], T.ab1[:], u, 0.25, OP.max, OP.is_lt)
     quant("qz", 0, 128, "zt", "ztv zt", "qz")
     mm(1, "qtri", 0, "qz", 128, "qtri qz")
+    ts("ab", "qoh", T.qoh[:], T.ab[:], 16.0, None, OP.is_lt)
+    ts("y1", "lo", lo, y1, -111.0, 16.0, OP.add, OP.min)
+    ts("y1", "hi", hi, y1, -127.0, 0.0, OP.add, OP.max)
     for k, (c, sc, rd) in enumerate(((0, T.pf[:, 0:1], "pm"), (1, T.pc[:, 0:1], "khi"), (32, lo, "lo"), (33, hi, "hi"))):
         act("qoh bt " + rd, "b%d" % k, T.bt[:, c:c // 32 * 32 + 32:4], T.qoh[:], AF.Copy, scale=sc)
-    quant("qb", 0, 128, "bt", "bt b0 b1 b2 b3", "qb")
     tt("ps1 ztv", "zc", T.zc[:], T.ps1[:, 0:8], T.zt[:, 0:32:4], OP.mult)
     op("V", "zc", "o1", V.tensor_reduce, o1, T.zc[:], X, OP.add)
+    quant("qb", 0, 128, "bt", "bt b0 b1 b2 b3", "qb")
     for t in range(2):
         ts("pm1 o1 att", "at%d" % t, T.att[:, t:512:4], T.pm1[:], o1, None, OP.is_equal)
     quant("qa", 0, 128, "att", "att at0 at1", "qa")
@@ -263,44 +286,29 @@ def rank_program(g, core, T, topo):
     pick("slots", CAPP * r, CAPP * r + CAPP, "qx", 128, "off", 0, 1, "qx off", "slown")
     act("lst", "lown", T.landL[:, 4 * r:4 * r + 1], T.lst[:, 0:1], AF.Copy)
 
-    fill("", "rs", T.rs[:], 1.0)
-    fill("rs", "rs", T.rs[:, 0:1], 0.0)
-    fill("rs", "rs", T.rs[:, 128:129], 0.0)
-    quant("slots", 128, 128, "zz", "zz zzb", "slz")
-    quant("pk", 64, 128, "zz", "zz zzb", "pkz")
-    fill("", "aw", T.aw[:], 0.0)
-    ts("row8 pm", "jw", T.jw[:], T.row8[:], 16.0, T.pf[:, 0:1], OP.mult, OP.add)
-    quant("qw", 0, 512, "wt", "wt", "qw")
-    fill("", "ar0", T.ar[:, 256:272], 0.0)
-    fill("", "fa", T.fa[:], 0.0)
-    for t in range(3):
-        ts("pm1 a0 ct", "ca%d" % t, T.ct[:, 512 + t:1024:4], T.pm1[:], T.pc[:, 1:2], None, OP.is_equal)
-    ts("row8 ph16", "m8", T.m8[:], T.row8[:], T.pf[:, 1:2], None, OP.is_equal)
-    ts("row16 ph16", "m16", T.m16[:], T.row16[:], T.pf[:, 1:2], None, OP.is_equal)
-    ts("jw", "jn", T.jn[:], T.jw[:], -1.0, 127.0, OP.mult, OP.add)
-    quant("qa2", 0, 128, "ct", "ct ca0 ca1 ca2", "qa2", at=512)
-    st2, st, pl, ph, q32, q128, mn, mgc = [T.sc[:, i:i + 1] for i in range(7, 15)]
     ts("o1", "st2", st2, o1, CAPP + 0.5, None, OP.is_lt)
-    ts("o1 st2", "st", st, o1, 0.5, st2, OP.is_gt, OP.mult)
-    ts("o1 st", "pl", pl, o1, -1.0, st, OP.add, OP.mult)
     ts("q2", "q32", q32, q2, 16.0, 112.0, OP.mult, OP.add)
-    ts("q2", "q128", q128, q2, 64.0, 448.0, OP.mult, OP.add)
+    ts("o1 st2", "st", st, o1, 0.5, st2, OP.is_gt, OP.mult)
+    ts("q2 best", "gn", gn, q2, 48.0, best, OP.mult, OP.add)
+    ts("o1 st", "pl", pl, o1, -1.0, st, OP.add, OP.mult)
     ts("q32 st", "ph", ph, q32, 16.0 * (r % 2) - 256.0, st, OP.add, OP.mult)
+    ts("gn", "gn", gn, gn, 337.0, None, OP.add)
     ts("ph", "ph", ph, ph, 256.0, None, OP.add)
-    for k, (c, n, m, sc, rd) in enumerate(((0, 16, "m16", pl, "pl"), (1, 16, "m16", ph, "ph"), (64, 8, "m8", lo, "lo"),
-                                           (65, 8, "m8", hi, "hi"), (66, 8, "m8", q32, "q32"), (96, 8, "m8", lo, "lo"),
-                                           (97, 8, "m8", hi, "hi"), (98, 8, "m8", q128, "q128"))):
-        ts(m + " b2t " + rd, "w%d" % k, T.b2t[:, c:c // 32 * 32 + 4 * n:4], T[m][:], sc, None, OP.mult)
-    quant("qb2", 0, 128, "b2t", "b2t " + " ".join("w%d" % k for k in range(8)), "qb2")
+    for k, (c, n, m, sc, rd) in enumerate(((64, 8, "m8", lo, "lo"), (65, 8, "m8", hi, "hi"), (66, 8, "m8", q32, "q32"),
+                                           (0, 16, "m16", pl, "pl"), (1, 16, "m16", ph, "ph"))):
+        act(m + " b2t " + rd, "w%d" % k, T.b2t[:, c:c // 32 * 32 + 4 * n:4], T[m][:], AF.Copy, scale=sc)
+    quant("qe", 0, 512, "et", "et0 et1 et2 et3 e0 e1 e2 e3", "qe")
+    for b in range(4):
+        mm(4 + b, "qe", 128 * b, "qx", 128, "qe qx")
+        act("ps%d" % (4 + b), "dan%d" % b, T.dan[:, 32 * b:32 * b + 32], T["ps%d" % (4 + b)][:, 0:A], AF.Copy)
+    quant("qb2", 0, 128, "b2t", "b2t w0 w1 w2 w3 w4", "qb2")
     mm(3, "qa2", 0, "qb2", 128, "qa2 qb2")
-    cp("ps3", "posD", T.posD[:], T.ps3[:, 0:16])
-    cp("ps3", "gw", T.gw[:], T.ps3[:, 16:32])
-    tt("gw jn", "tmp", T.tmp[:], T.gw[:, 0:8], T.jn[:], OP.add)
+    quant("qw", 0, 512, "wt", "wt", "qw")
 
     for c in range(4):
         la, lb = T.landL[:, 8 * c:8 * c + 1], T.landL[:, 8 * c + 4:8 * c + 5]
         if c < 2:
-            ts("landL lown zz", "lx%d" % c, T.lx[:, 32 * c:32 * c + 32], T.zz[:, 0:32], la, lb, OP.add, OP.add)
+            ts("landL lown zz0", "lx%d" % c, T.lx[:, 32 * c:32 * c + 32], T.zz[:, 0:32], la, lb, OP.add, OP.add)
         else:
             act("landL lown ones", "lx%d" % c, T.lx[:, 32 * c:32 * c + 32], T.ones[:, 0:32], AF.Identity, bias=lb, scale=la)
     op("V", "lx0 lx1 lx2 lx3", "arow", V.transpose, T.arow[:], T.lx[:])
@@ -314,10 +322,6 @@ def rank_program(g, core, T, topo):
     for h in range(2):
         op("V", "c2", "F%d" % (2 + h), V.tensor_reduce, T.F4[:, 2 + h:3 + h], T.c2[:, 128 * h:128 * h + 128], X, OP.add)
     cp("F0 F1 F2 F3", "fs", T.fs[:], T.F4[:])
-
-    pick("pk", 0, 64, "slots", 256, "fs", 0, 4, "slots slown slowns slz fs", "pk")
-    for b in range(4):
-        mm(4 + b, "qe", 128 * b, "pk", 128, "qe pk pks pkz")
     ts("F0 F1 F2 F3", "n1", T.n1[:], T.F4[:], 127.5, None, OP.is_gt)
     tt("n1 jw", "n2", T.n2[:], T.n1[:], T.jw[:, 0:4], OP.mult)
     tt("n2 F0 F1 F2 F3", "n3", T.n3[:], T.n2[:], T.F4[:], OP.add)
@@ -326,6 +330,13 @@ def rank_program(g, core, T, topo):
     op("V", "aws", "at", V.transpose, T.at[:], T.aw[:, 0:128])
     cp("at", "adm4", T.adm4[:, 0:4], T.at[:, 0:128:32])
     to_all("adm4", T.adm4[:, 0:4], T.land3[:, 8 * r:8 * r + 4], "m3", "o3a")
+
+    pick("pk", 0, 64, "slots", 256, "fs", 0, 4, "slots slown slowns slz fs", "pk")
+    for b in range(4):
+        mm(4 + b, "qe", 128 * b, "pk", 128, "qe pk pks pkz")
+    ts("F0 F1", "jf0", T.jf[:, 0:2], T.F4[:, 0:2], 127.5, 128.0 + A * r, OP.is_lt, OP.mult)
+    cp("jw", "jf2", T.jf[:, 2:8], T.jw[:, 2:8])
+    tt("jf0 jw", "jf1", T.jf[:, 0:2], T.jf[:, 0:2], T.jw[:, 0:2], OP.add)
     for k in range(5):
         if k < 4:
             tt("ps%d dan%d" % (4 + k, k), "tb%d" % k, T.tb[:, 32 * k:32 * k + 32], T["ps%d" % (4 + k)][:, 0:A],
@@ -335,9 +346,11 @@ def rank_program(g, core, T, topo):
             tt("ps%d tb%d mt" % (4 + b, b), "mt%d" % b, T.mt[:, b:4 * A:4], T["ps%d" % (4 + b)][:, A:2 * A],
                T.tb[:, 32 * b:32 * b + 32], OP.add)
     quant("km", 0, 128, "mt", "mt mt0 mt1 mt2 mt3", "km")
+    cp("ps3", "posD", T.posD[:], T.ps3[:, 0:16])
+    tt("ps3 jn", "tmp", T.tmp[:], T.ps3[:, 16:24], T.jn[:], OP.add)
     for i in range(4):
         mm(i, "qw", 128 * i, "km", 128, "qw km")
-        layer(i, "ht", A, "ht%d" % i, "ht")
+        layer(i, "ht", A, "ht%d" % i, "ht", True)
     quant("hq", 0, 128, "ht", "ht ht0 ht1 ht2 ht3", "hq")
 
     to_all("hq", T.hq[:, 0:A].bitcast(dt.uint8), T.hw[:, 128 + A * r:128 + A * r + A].bitcast(dt.uint8), "h3", "o3b")
@@ -345,30 +358,28 @@ def rank_program(g, core, T, topo):
     arrive("m3", width * (N - 1), "land3")
     arrive("h3", 2 * width * (N - 1), "hwr")
     cp("at", "adown", T.land3[:, 8 * r:8 * r + 4], T.at[:, 0:128:32])
-    for i in range(4):
-        mm(i, "qw", 128 * i, "qx", 128, "qw qx")
-        layer(i, "hot", 128, "ho%d" % i)
-    quant("hw", 0, 128, "hot", "ho0 ho1 ho2 ho3", "hwo")
     pick("hw", 128 + A * r, 128 + A * r + A, "hq", 128, "il", 0, 2, "hq il0 il1", "hwn")
     quant("qv", 0, 128, "vt", "vt", "qv")
-    ts("fa F0 F1", "fav", T.fa[:, 0:2], T.F4[:, 0:2], 127.5, 128.0 + A * r, OP.is_lt, OP.mult)
-    tt("fa fav jw", "jf", T.jf[:], T.fa[:], T.jw[:], OP.add)
+    fill("", "ar0", T.ar[:, 256:272], 0.0)
+    for i in range(4):
+        mm(i, "qw", 128 * i, "qx", 128, "qw qx")
+        layer(i, "hot", 128, "ho%d" % i, "", False)
+    quant("hw", 0, 128, "hot", "ho0 ho1 ho2 ho3", "hwo")
     for q in range(N):
         col = T.land3[:, 8 * q + r // 2:8 * q + r // 2 + 1]
         if q % 2:
             ts("land3 adown ones", "ax%d" % q, T.ax[:, 32 * q:32 * q + 32], T.ones[:, 0:32], 0.0, col, OP.mult, OP.add)
         else:
-            act("land3 adown zz", "ax%d" % q, T.ax[:, 32 * q:32 * q + 32], T.zz[:, 0:32], AF.Identity, bias=col)
+            act("land3 adown zz0", "ax%d" % q, T.ax[:, 32 * q:32 * q + 32], T.zz[:, 0:32], AF.Identity, bias=col)
     op("V", " ".join("ax%d" % q for q in range(N)), "ar", V.transpose, T.ar[:, 0:256], T.ax[:])
     cp("ar ar0 posD", "aj", T.aj[:], T.ar[:, 0:272].indirect(T.posD[:, 0:16]))
     op("V", "aj", "ajt", V.transpose, T.ajt[:], T.aj[:])
     tt("ajt tmp", "f1", T.f1[:], T.ajt[:, 0:256:32], T.tmp[:], OP.mult)
-    tt("f1 jf", "f2", T.f2[:], T.f1[:], T.jf[:], OP.add)
+    tt("f1 jf1 jf2", "f2", T.f2[:], T.f1[:], T.jf[:], OP.add)
     cp("f2", "fin", T.fin[:], T.f2[:])
-    tt("ajt gw", "mw", T.mw[:], T.ajt[:, 0:256:32], T.gw[:, 8:16], OP.mult)
-    tt("mw m8", "mw2", T.mw2[:], T.mw[:], T.m8[:], OP.mult)
+    tt("ajt m8", "mw2", T.mw2[:], T.ajt[:, 0:256:32], T.m8[:], OP.mult)
     op("V", "mw2", "mn", V.tensor_reduce, mn, T.mw2[:], X, OP.add)
-    ts("mn", "mgc", mgc, mn, -1.0, None, OP.add)
+    ts("mn gn", "mgc", mgc, mn, gn, -1.0, OP.mult, OP.add)
     dma("S", "mgc", "mgo", T.mg[:], mgc)
 
     pick("fo", 0, 128, "hw", 384, "fin", 0, 8, "hwo hwr hwn hwns fin", "fo")

@@ -14,20 +14,23 @@ def _mx(name, cols):
     _buf(name + "s", cols, U8)
 
 
-for _n, _c in (("qx", 128), ("qn", 128), ("anc", 288), ("qtri", 128), ("qa2", 128), ("qe", 512), ("qz", 128), ("qb", 128),
-               ("qa", 128), ("qb2", 128), ("snd", 128), ("slots", 256), ("pk", 192), ("qw", 512), ("qv", 128), ("km", 128),
+for _n, _c in (("qx", 128), ("qn", 128), ("anc", 288), ("qtri", 128), ("qa2", 128), ("qe", 512), ("qz", 128), ("qab", 144),
+               ("qb2", 128), ("snd", 128), ("slots", 256), ("pk", 192), ("qw", 512), ("qv", 128), ("km", 128),
                ("hq", 128), ("hw", 384), ("fo", 128)):
     _mx(_n, _c)
-for _n, _c in (("xt", 512), ("xa", 512), ("wt", 2048), ("vt", 512), ("ct", 1024), ("et", 2048), ("zt", 512), ("bt", 512),
-               ("att", 512), ("b2t", 512), ("zz", 512), ("mt", 512), ("ht", 512), ("hot", 512), ("ones", 128), ("ident", 128),
-               ("tri", 128), ("pm1", 128), ("rs", 256), ("lx", 128), ("arow", 128), ("eq", 256), ("cc", 256), ("c2", 256),
+_buf("rl", 64, MXC)
+_buf("rms", 64, U8)
+_buf("rhs", 32, U8)
+for _n, _c in (("xt", 512), ("xa", 512), ("wt", 2048), ("vt", 512), ("ct", 512), ("ct2", 512), ("et", 516), ("ztb", 608),
+               ("att", 576), ("zz", 512), ("mz", 640), ("hot", 512), ("ones", 128), ("ident", 128),
+               ("tri", 128), ("pm1", 256), ("lx", 128), ("arow", 128), ("eq", 256), ("cc", 256), ("c2", 256),
                ("j12", 256), ("aw", 192), ("at", 128), ("adm4", 8), ("land3", 64), ("ax", 256), ("ar", 272), ("aj", 256),
                ("ajt", 256)):
     _buf(_n, _c, BF)
-for _n, _c in (("z32", 288), ("R", 288), ("mrow", 96), ("thr", 96), ("t1", 96), ("t2", 97), ("sc", 16), ("jr", 256), ("j7", 8),
-               ("ab", 8), ("ab1", 8), ("qoh", 8), ("zc", 8), ("qi", 8), ("qc", 8), ("ri", 8), ("qh", 8), ("crow", 32),
-               ("row8", 8), ("row16", 16), ("pf", 4), ("pc", 8), ("m8", 8), ("m16", 16), ("jw", 8), ("jn", 8), ("lst", 8),
-               ("landL", 32), ("F4", 4), ("dan", 128), ("tb", 128), ("n1", 4), ("n2", 4), ("n3", 4), ("tmp", 8),
+for _n, _c in (("R", 288), ("mrow", 32), ("thr", 64), ("t1", 64), ("t2", 97), ("sc", 16), ("jr", 256),
+               ("j7", 16), ("ab", 32), ("pen", 32), ("msk", 32), ("num", 32), ("qi", 8), ("qc", 32), ("ri", 16), ("qh", 16),
+               ("crow", 32), ("row8", 8), ("row16", 16), ("pf", 4), ("pc", 8), ("m8", 8), ("m16", 16), ("jw", 8), ("jn", 8),
+               ("lst", 8), ("landL", 32), ("F4", 4), ("tb", 128), ("n1", 4), ("n2", 4), ("n3", 4), ("tmp", 8),
                ("jf", 8), ("f1", 8), ("f2", 8), ("mw2", 8), ("yo", 128)):
     _buf(_n, _c, F32)
 for _n, _c in (("il", 2), ("off", 8), ("fs", 4), ("sof", 4), ("posD", 16), ("fin", 8)):
@@ -36,16 +39,61 @@ _buf("pi", 1, I32)
 _buf("pin", 4, I32)
 for _i in range(8):
     SCRATCH["ps%d" % _i] = ("psum", [128, 512], F32)
-SEMAPHORES = (["cV", "cA", "cP", "cG", "a1", "o1s", "l2", "c2r", "o2a", "o2b", "m3", "o3a", "h3", "o3b"]
-              + ["d%d" % _i for _i in range(12)])
+SEMAPHORES = (["cV", "cA", "cP", "cG", "a1", "o1s", "l2", "c2r", "o2a", "o2b", "o2c", "m3", "o3a", "h3", "o3b", "o3c",
+               "rc", "rp", "rk", "hl"] + ["d%d" % _i for _i in range(12)])
+
+
+def to(topo, c):
+    return DstId(rid=topo.addr(c)[0], pnc=topo.addr(c)[1])
+
+
+def plan(own, r, T, topo):
+    for b in ((2, 1, 0), (0, 2, 1), (1, 2, 0)):
+        order = [r ^ sum((c >> (2 - i) & 1) << b[i] for i in range(3)) for c in range(8)]
+        if all(topo.same_plane(topo.chip(own), topo.chip(T.cores[q])) for q in order[1:4]):
+            break
+    near, far = [T.cores[q] for q in order[1:4]], [T.cores[q] for q in order[4:]]
+    rest = sorted([c for c in topo.cores_of(own) if c != own], key=lambda c: topo.die(c) == topo.die(own))
+    f = [c for c in rest if all(topo.may_write(c, d) for d in far)][:2]
+    n = [c for c in rest if c not in f and all(topo.may_write(c, d) for d in near)][:2]
+    return order, near, far, [f[0], n[0], f[1], n[1]]
+
+
+def hand_on(g, core, r, role, near, far, T, topo):
+    S, CAPP, A = T.sem, 16, 32
+    goal, first = (near, 1) if role % 2 else (far, 0)
+    eng = topo.engines(core, goal[0])
+
+    def piece(i):
+        a = CAPP * (i + first)
+        return T.rms[:, a:a + CAPP] if role >= 2 else T.rl[:, a:a + CAPP].bitcast(dt.uint8)
+
+    land = T.slotss[:, CAPP * r:CAPP * r + CAPP] if role >= 2 else T.slots[:, CAPP * r:CAPP * r + CAPP].bitcast(dt.uint8)
+    g.wait_ge(S.rp if role >= 2 else S.rc, 4)
+    g.remote_dma_fused([RemoteDMATransfer(dst_ids=[to(topo, d)], dma_engine_mask=1 << eng[2 * i] | 1 << eng[2 * i + 1],
+                                          remote_sem=S.c2r, src=piece(i), dst=land) for i, d in enumerate(goal)], local_sem=S.hl)
+    n = 2 * len(goal)
+    if role >= 2:
+        g.wait_ge(S.rk, 4)
+        g.remote_dma_fused([RemoteDMATransfer(dst_ids=[to(topo, d) for d in goal], dma_engine_mask=topo.mask(core, goal[0]),
+                                              remote_sem=S.h3, srcs=[T.rhs[:, 0:A]],
+                                              dsts=[T.hws[:, 128 + A * r:128 + A * r + A]] * len(goal))], local_sem=S.hl)
+        n += len(eng)
+    g.wait_ge(S.hl, n)
 
 
 def rank_program(g, core, T, topo):
-    r = T.rank_of(core)
-    if r is None:
-        return
     N, S = len(T.cores), T.sem
     A, CAPP, KM = 32, 16, 48
+    mine = [c for c in T.cores if topo.chip(c) == topo.chip(core)]
+    if not mine:
+        return
+    r = T.rank_of(mine[0])
+    order, near, far, help4 = plan(mine[0], r, T, topo)
+    if core != mine[0]:
+        if core in help4:
+            hand_on(g, core, r, help4.index(core), near, far, T, topo)
+        return
     OP, AF, X = AluOpType, ActivationFunctionType, AxisListType.X
     V, AC, PE, SY = g.vector, g.scalar, g.tensor, g.sync
     tiny = 1e-29
@@ -102,27 +150,35 @@ def rank_program(g, core, T, topo):
         count[s] = n
         after((s, n, {}), [], wr.split())
 
-    order = [r ^ c for c in range(N)]
     others = [T.cores[q] for q in order[1:]]
-    dst = {c: DstId(rid=topo.addr(c)[0], pnc=topo.addr(c)[1]) for c in others}
     allm = topo.mask(core, others[0])
     for c in others:
         allm &= topo.mask(core, c)
     eng = [e for e in topo.engines(core, others[0]) if allm >> e & 1]
     width = len(eng)
+    side = [e for e in topo.engines(core, help4[0]) if e not in eng]
 
     def to_all(rd, src, dstap, sem, loc):
         before("G", rd.split(), [])
-        g.remote_dma_fused([RemoteDMATransfer(dst_ids=[dst[c] for c in others], dma_engine_mask=allm, remote_sem=S[sem],
+        g.remote_dma_fused([RemoteDMATransfer(dst_ids=[to(topo, c) for c in others], dma_engine_mask=allm, remote_sem=S[sem],
                                               srcs=[src], dsts=[dstap] * len(others))], local_sem=S[loc])
         count[loc] = count.get(loc, 0) + width
 
     def to_each(rd, src, dstap, sem, loc):
         before("G", rd.split(), [])
-        g.remote_dma_fused([RemoteDMATransfer(dst_ids=[dst[others[c - 1]]], dma_engine_mask=1 << eng[c - 1],
+        g.remote_dma_fused([RemoteDMATransfer(dst_ids=[to(topo, others[c - 1])], dma_engine_mask=1 << eng[c - 1],
                                               remote_sem=S[sem], src=src(c), dst=dstap) for c in range(1, N)],
                            local_sem=S[loc])
         count[loc] = count.get(loc, 0) + N - 1
+
+    def to_two(rd, src, dstap, sem, loc, roles):
+        before("G", rd.split(), [])
+        h = len(side) // 2
+        g.remote_dma_fused([RemoteDMATransfer(dst_ids=[to(topo, help4[k])],
+                                              dma_engine_mask=sum(1 << e for e in side[h * i:h * i + h]),
+                                              remote_sem=S[sem], src=src[i], dst=dstap) for i, k in enumerate(roles)],
+                           local_sem=S[loc])
+        count[loc] = count.get(loc, 0) + 2 * h
 
     def ts(rd, wr, out, in0, s1, s2, *ops):
         op("V", rd, wr, V.tensor_scalar, out, in0, s1, s2, *ops)
@@ -142,187 +198,171 @@ def rank_program(g, core, T, topo):
     def iota(wr, out, pattern, base=0, mult=0):
         op("G", "", wr, g.iota, out, pattern, base, mult, allow_small_or_imprecise_dtypes=True)
 
-    def mm(bank, w, wv, x, n, rd):
+    def mm(bank, w, wv, x, n, rd, xv=0, start=True, stop=True):
         op("P", rd, "ps%d" % bank, PE.matmul_mx, T["ps%d" % bank][:, 0:n], T[w][:, wv:wv + 128], T[w + "s"][:, wv:wv + 128],
-           T[x][:, 0:n], T[x + "s"][:, 0:n], True, True)
+           T[x][:, xv:xv + n], T[x + "s"][:, xv:xv + n], start, stop)
 
     def quant(out, a, n, tile, rd, wr, at=0):
         op("V", rd, wr, V.quantize_mx, T[out][:, a:a + n], T[out + "s"][:, a:a + n], T[tile][:, at:at + 4 * n])
 
-    def pick(out, a, b, win, w, lists, la, lb, rd, wr):
-        cp(rd, wr, T[out][:, a:b].bitcast(dt.uint32), T[win][:, 0:w].bitcast(dt.uint32).indirect(T[lists][:, la:lb]))
-        act(rd, wr + "s", T[out + "s"][:, a:b], T[win + "s"][:, 0:w].indirect(T[lists][:, la:lb]), AF.Copy)
+    def pick(out, a, b, win, w, lists, la, lb, rd, wr, at=0):
+        cp(rd, wr, T[out][:, a:b].bitcast(dt.uint32), T[win][:, at:w].bitcast(dt.uint32).indirect(T[lists][:, la:lb]))
+        act(rd, wr + "s", T[out + "s"][:, a:b], T[win + "s"][:, at:w].indirect(T[lists][:, la:lb]), AF.Copy)
 
-    def layer(i, tile, n, wr, rd, both):
-        src, out = T["ps%d" % i][:, 0:n], T[tile][:, i:4 * n:4]
+    def layer(i, tile, a, n, wr, both):
+        src, out = T["ps%d" % i][:, 0:n], T[tile][:, a + i:a + 4 * n:4]
         if i % 2 and both:
-            ts("ps%d " % i + rd, wr, out, src, 0.0, 0.0625, OP.max, OP.mult)
+            ts("ps%d" % i, wr, out, src, 0.0, 0.0625, OP.max, OP.mult)
         else:
-            act("ps%d " % i + rd, wr, out, src, AF.Relu, scale=0.0625)
+            act("ps%d" % i, wr, out, src, AF.Relu, scale=0.0625)
 
     dma("S", "", "xa", T.xa[:, 0:4 * A], T.x[:, 0:4 * A])
     dma("S", "", "xt", T.xt[:], T.x[:])
-    sg = [-1 if r >> b & 1 else 1 for b in (2, 1, 0)]
     op("G", "", "pi", g.iota, T.pi[:], [[0, 1]], 0, 1)
-    iota("qi", T.qi[:], [[4 * A * sg[0], 2], [2 * A * sg[1], 2], [A * sg[2], 2]], A * r)
-    iota("ri", T.ri[:], [[A, 8]])
-    iota("crow", T.crow[:], [[1, 32]])
-    fill("", "z32", T.z32[:], 0.0)
+    iota("qi", T.qi[:], [[A * (order[c] - r), 2] for c in (4, 2, 1)], A * r)
     fill("", "ones", T.ones[:], 1.0)
-    fill("", "xaz", T.xa[:, 4 * A:], 0.0)
-    ts("pi", "pin", T.pin[:, 0:1], T.pi[:], 15, None, OP.bitwise_and)
-    ts("pin", "il0", T.il[:, 0:1], T.pin[:, 0:1], 0, None, OP.add)
-    ts("pin", "il1", T.il[:, 1:2], T.pin[:, 0:1], 16, None, OP.add)
     op("G", "ones", "tri", g.affine_select, T.tri[:], T.ones[:], [[1, 128]], OP.is_ge, 0.0, 0, -1)
-    for h in range(2):
-        act("z32", "zz%d" % h, T.zz[:, 256 * h:256 * h + 256], T.z32[:, 0:256], AF.Copy)
-    for k in ("mt", "ht"):
-        act("zz0 zz1", k, T[k][:], T.zz[:], AF.Copy)
-    for b in range(4):
-        act("zz0 zz1", "et%d" % b, T.et[:, 512 * b:512 * b + 512], T.zz[:], AF.Copy)
-    for k in ("zt", "att", "bt"):
-        fill("", k, T[k][:], 0.0)
-
+    fill("", "xaz", T.xa[:, 4 * A:], 0.0)
+    fill("", "zz", T.zz[:], 0.0)
+    ts("pi", "pin", T.pin[:, 0:1], T.pi[:], 15, None, OP.bitwise_and)
     quant("qn", 0, 128, "xa", "xa xaz", "qn")
+
     to_all("qn", T.qn[:, 0:A].bitcast(dt.uint8), T.anc[:, A * r:A * r + A].bitcast(dt.uint8), "a1", "o1s")
     to_all("qn", T.qns[:, 0:A], T.ancs[:, A * r:A * r + A], "a1", "o1s")
     arrive("a1", 2 * width * (N - 1), "anc")
-    for a, k in ((A * r, "own"), (N * A, "pad")):
-        pick("anc", a, a + A, "qn", 128, "il", 0, 2, "qn il0 il1", "anc" + k)
-    quant("qx", 0, 128, "xt", "xt", "qx")
     SY.wait_ge(S.o1s, 2 * width)
     known["S"]["o1s"] = 2 * width
     dma("S", "", "wt", T.wt[:], T.w[:])
     dma("S", "", "vt", T.vt[:], T.v[:])
 
     op("G", "ones", "ident", g.affine_select, T.ident[:], T.ones[:], [[1, 128]], OP.is_equal, 0.0, 0, -1)
-    iota("pm1", T.pm1[:], [[0, 8], [1, 16]], 1)
+    iota("ri", T.ri[:, 0:15], [[A, 15]], -7 * A)
+    iota("crow", T.crow[:], [[1, 32]])
+    iota("pm1", T.pm1[:], [[0, 8], [1, 16], [0, 2]], 65)
     iota("row8", T.row8[:], [[1, 8]])
     iota("row16", T.row16[:], [[1, 8], [0, 2]])
-    iota("b2t", T.b2t[:], [[0, 512]])
+    for k in range(4):
+        act("qi", "qc%d" % k, T.qc[:, k // 2 * 16 + k % 2:k // 2 * 16 + 16:2], T.qi[:], AF.Identity, bias=0.5 * A - 0.5)
+    act("zz", "num3", T.num[:, 17:32:2], T.zz[:, 0:8], AF.Identity, bias=32.0)
+    ts("pin", "il0", T.il[:, 0:1], T.pin[:, 0:1], 0, None, OP.add)
+    ts("pin", "il1", T.il[:, 1:2], T.pin[:, 0:1], 16, None, OP.add)
     fill("", "ct", T.ct[:], 0.0)
-    act("tri ct", "ctri", T.ct[:, 0:512:4], T.tri[:], AF.Copy)
+    for a, k in ((A * r, "own"), (N * A, "pad")):
+        pick("anc", a, a + A, "qn", 128, "il", 0, 2, "qn il0 il1", "anc" + k)
     ts("pi", "pin1", T.pin[:, 1:2], T.pi[:], 4, None, OP.arith_shift_right)
     ts("pi", "pin2", T.pin[:, 2:3], T.pi[:], 31, None, OP.bitwise_and)
     cp("pin", "pm", T.pf[:, 0:1], T.pin[:, 0:1])
     cp("pin1", "ph16", T.pf[:, 1:2], T.pin[:, 1:2])
     cp("pin2", "p31", T.pf[:, 2:3], T.pin[:, 2:3])
-    ts("crow p31", "thr0", T.thr[:, 0:32], T.crow[:], T.pf[:, 2:3], -tiny, OP.is_lt, OP.mult)
-    fill("", "thr1", T.thr[:, 32:96], 0.0)
-    fill("thr1", "thr2", T.thr[64:128, 64:96], -tiny)
-    fill("thr2", "thr3", T.thr[96:128, 32:64], -tiny)
-    fill("", "kk", T.t2[:, 96:97], 0.5 - KM)
+    act("tri ct", "ctri", T.ct[:, 0:512:4], T.tri[:], AF.Copy)
+    act("ident ct", "cid", T.ct[:, 2:512:4], T.ident[:], AF.Copy, scale=64.0)
+    act("zz pm", "num0", T.num[:, 0:16:2], T.zz[:, 0:8], AF.Identity, bias=T.pf[:, 0:1])
+    act("ph16", "khi", T.pc[:, 0:1], T.pf[:, 1:2], AF.Copy, scale=16.0)
+    quant("qx", 0, 128, "xt", "xt", "qx")
+    act("zz khi", "num1", T.num[:, 1:16:2], T.zz[:, 0:8], AF.Identity, bias=T.pc[:, 0:1])
+    act("pm", "a0", T.pc[:, 1:2], T.pf[:, 0:1], AF.Identity, bias=16.0)
+    act("pm", "a1c", T.pc[:, 2:3], T.pf[:, 0:1], AF.Identity, bias=32.0)
+    act("pm", "a65", T.pc[:, 4:5], T.pf[:, 0:1], AF.Identity, bias=65.0)
+    ts("crow p31", "thr0", T.thr[:, 0:32], T.crow[:], T.pf[:, 2:3], tiny, OP.is_lt, OP.mult)
+    fill("", "thr1", T.thr[:, 32:64], 0.0)
+    fill("", "kk", T.t2[:, 96:97], 16.0 - KM + 0.5)
+    fill("", "t10", T.t1[0:32, 32:64], 0.0)
+    fill("", "t20", T.t2[0:32, 64:96], 0.0)
+    fill("thr1", "thr2", T.thr[96:128, 32:64], tiny)
     fill("kk", "kk", T.t2[0:32, 96:97], 1000.0)
-    fill("", "mq0", T.mrow[0:32, 32:96], 0.0)
-    ts("qi", "qc", T.qc[:], T.qi[:], 0.5 * A - 0.5, None, OP.add)
-    ts("ri", "qh", T.qh[:], T.ri[:], -0.5, None, OP.add)
-    ts("ph16", "khi", T.pc[:, 0:1], T.pf[:, 1:2], 16.0, None, OP.mult)
-    ts("pm", "a0", T.pc[:, 1:2], T.pf[:, 0:1], 1.0, None, OP.add)
-    ts("pm", "a1c", T.pc[:, 2:3], T.pf[:, 0:1], 17.0, None, OP.add)
+    ts("ri", "qh", T.qh[:, 0:15], T.ri[:, 0:15], -0.5, None, OP.add)
+    quant("qtri", 0, 128, "ct", "ctri cid ct", "qtri")
+    fill("", "ztb", T.ztb[:], 0.0)
+    fill("", "att", T.att[:], 0.0)
     ts("p31", "hp", T.pc[:, 3:4], T.pf[:, 2:3], 15.5, float(r % 2), OP.is_gt, OP.is_equal)
-    quant("qtri", 0, 128, "ct", "ctri ct", "qtri")
-    for b in range(4):
-        act("ident et%d" % b, "e%d" % b, T.et[:, 512 * b + b:512 * b + 512:4], T.ident[:], AF.Copy, scale=0.5)
-    fill("", "rs", T.rs[:], 1.0)
-    fill("rs", "rs", T.rs[:, 0:1], 0.0)
-    fill("rs", "rs", T.rs[:, 128:129], 0.0)
-    quant("slots", 128, 128, "zz", "zz0 zz1", "slz")
-    quant("pk", 64, 128, "zz", "zz0 zz1", "pkz")
-    fill("", "aw", T.aw[:], 0.0)
-    ts("row8 pm", "jw", T.jw[:], T.row8[:], 16.0, T.pf[:, 0:1], OP.mult, OP.add)
-    ts("jw", "jn", T.jn[:], T.jw[:], -1.0, 127.0, OP.mult, OP.add)
-    ts("row8 ph16", "m8", T.m8[:], T.row8[:], T.pf[:, 1:2], None, OP.is_equal)
-    ts("row16 ph16", "m16", T.m16[:], T.row16[:], T.pf[:, 1:2], None, OP.is_equal)
-    for t in range(3):
-        ts("pm1 a0 ct", "ca%d" % t, T.ct[:, 512 + t:1024:4], T.pm1[:], T.pc[:, 1:2], None, OP.is_equal)
-    quant("qa2", 0, 128, "ct", "ct ca0 ca1 ca2", "qa2", at=512)
 
-    best, q2, y1, lo, hi, u, o1, st2, st, pl, ph, q32, gn, mn, mgc = [T.sc[:, i:i + 1] for i in range(15)]
+    fill("", "et", T.et[:], 0.0)
+    act("ident et", "e", T.et[:, 4:516:4], T.ident[:], AF.Copy, scale=0.5)
+    act("row8 pm", "jw", T.jw[:], T.row8[:], AF.Identity, scale=16.0, bias=T.pf[:, 0:1])
+    act("jw", "jn", T.jn[:], T.jw[:], AF.Identity, scale=-1.0, bias=144.0)
+    quant("slots", 128, 128, "zz", "zz", "slz")
+    quant("pk", 64, 128, "zz", "zz", "pkz")
+
+    best, q2, d16, u, o1, st2, st, pl, ph, q32, gn, mn, mgc = [T.sc[:, i:i + 1] for i in range(13)]
     M = T.R[:, 255:256]
-    mm(0, "qx", 0, "anc", 288, "qx anc ancown ancowns ancpad ancpads")
-    op("V", "ps0 z32", "R", V.tensor_tensor_scan, T.R[:], T.ps0[:, 0:288], T.z32[:], -9.0e29, OP.max, OP.add)
-    op("V", "R", "m0", V.transpose, T.mrow[:, 0:32], T.R[:, 256:288])
-    for a in range(1, 4):
-        for k in (1, 2):
-            b = (a - 1 + k) % 3 + 1
-            to, of = T.mrow[32 * a:32 * a + 32, 32 * k:32 * k + 32], T.mrow[32 * b:32 * b + 32, 0:32]
-            if k == 1:
-                cp("m0", "m%d%d" % (a, k), to, of)
-            else:
-                act("m0", "m%d%d" % (a, k), to, of, AF.Copy)
-    act("R", "best jr", T.jr[:], T.R[:, 0:256], AF.Sign, bias=M, scale=-1.0, accum_out=best)
-    act("best qc", "ab", T.ab[:], T.qc[:], AF.Abs, bias=best, scale=-1.0)
-    act("ab", "ab1", T.ab1[:], T.ab[:], AF.Copy, scale=1.0 / 64)
-    act("best qh", "q2 j7", T.j7[:, 0:7], T.qh[:, 1:8], AF.Sign, bias=best, scale=-1.0, accum_out=q2)
-    act("q2 best", "y1", y1, q2, AF.Identity, bias=best, scale=-16.0)
-    ts("R m0 mq0 m11 m12 m21 m22 m31 m32", "t1", T.t1[:], T.mrow[:], M, None, OP.subtract)
-    tt("t1 thr0 thr1 thr2 thr3", "t2", T.t2[:, 0:96], T.t1[:], T.thr[:], OP.is_gt)
-    op("V", "t2 kk", "u", V.tensor_reduce, u, T.t2[:], X, OP.add)
-    ts("ab1 u zt", "ztv", T.zt[:, 0:32:4], T.ab1[:], u, 0.25, OP.max, OP.is_lt)
-    quant("qz", 0, 128, "zt", "ztv zt", "qz")
-    mm(1, "qtri", 0, "qz", 128, "qtri qz")
-    ts("ab", "qoh", T.qoh[:], T.ab[:], 16.0, None, OP.is_lt)
-    ts("y1", "lo", lo, y1, -111.0, 16.0, OP.add, OP.min)
-    ts("y1", "hi", hi, y1, -127.0, 0.0, OP.add, OP.max)
-    for k, (c, sc, rd) in enumerate(((0, T.pf[:, 0:1], "pm"), (1, T.pc[:, 0:1], "khi"), (32, lo, "lo"), (33, hi, "hi"))):
-        act("qoh bt " + rd, "b%d" % k, T.bt[:, c:c // 32 * 32 + 32:4], T.qoh[:], AF.Copy, scale=sc)
-    tt("ps1 ztv", "zc", T.zc[:], T.ps1[:, 0:8], T.zt[:, 0:32:4], OP.mult)
-    op("V", "zc", "o1", V.tensor_reduce, o1, T.zc[:], X, OP.add)
-    quant("qb", 0, 128, "bt", "bt b0 b1 b2 b3", "qb")
-    for t in range(2):
-        ts("pm1 o1 att", "at%d" % t, T.att[:, t:512:4], T.pm1[:], o1, None, OP.is_equal)
-    quant("qa", 0, 128, "att", "att at0 at1", "qa")
-    mm(2, "qa", 0, "qb", 128, "qa qb")
+    mm(0, "qx", 0, "anc", 128, "qx anc ancown ancowns ancpad ancpads")
+    mm(1, "qx", 0, "anc", 160, "qx anc ancown ancowns ancpad ancpads", xv=128)
+    op("V", "ps0 zz", "R0", V.tensor_tensor_scan, T.R[:, 0:128], T.ps0[:, 0:128], T.zz[:, 0:128], -9.0e29, OP.max, OP.add)
+    op("V", "ps1 zz R0", "R", V.tensor_tensor_scan, T.R[:, 128:288], T.ps1[:, 0:160], T.zz[:, 0:160], T.R[:, 127:128],
+       OP.max, OP.add)
+    op("V", "R", "m0", V.transpose, T.mrow[:], T.R[:, 256:288])
 
-    cp("ps2", "off", T.off[:], T.ps2[:, 0:8])
-    act("ps2 hp", "lst", T.lst[:], T.ps2[:, 8:16], AF.Copy, scale=T.pc[:, 3:4])
+    def quad(t, q, c):
+        return T[t][32 * q:32 * q + 32, c:c + 32]
+
+    ts("R m0", "t1a", T.t1[:, 0:32], T.mrow[:], M, -1.0, OP.subtract, OP.mult)
+    for a in range(1, 4):
+        Ma = T.R[32 * a:32 * a + 32, 255:256]
+        b = a % 3 + 1
+        act("R m0", "t1%d" % a, quad("t1", a, 32), quad("mrow", b, 0), AF.Identity, scale=-1.0, bias=Ma)
+        b = (a + 1) % 3 + 1
+        ts("R m0", "t2%d" % a, quad("t2", a, 64), quad("mrow", b, 0), Ma, None, OP.is_ge if b < a else OP.is_gt)
+    act("R", "best jr", T.jr[:], T.R[:, 0:256], AF.Sign, bias=M, scale=-1.0, accum_out=best)
+    act("best qc0 qc1 qc2 qc3", "ab", T.ab[:], T.qc[:], AF.Abs, bias=best, scale=-1.0)
+    act("best qh", "q2 j7", T.j7[:, 0:15], T.qh[:, 0:15], AF.Sign, bias=best, scale=-1.0, accum_out=q2)
+    act("ab", "pen", T.pen[:], T.ab[:], AF.Relu, scale=-2.0, bias=32.0)
+    act("q2 best", "d16", d16, q2, AF.Identity, bias=best, scale=-16.0)
+    act("pen", "msk", T.msk[:], T.pen[:], AF.Sign)
+    act("d16 zz", "num2", T.num[:, 16:32:2], T.zz[:, 0:8], AF.Identity, bias=d16)
+    tt("t1a t11 t12 t13 t10 thr0 thr1 thr2", "t2", T.t2[:, 0:64], T.t1[:], T.thr[:], OP.is_lt)
+    op("V", "t2 t20 t21 t22 t23 kk", "u", V.tensor_reduce, u, T.t2[:], X, OP.add)
+    ts("ab u ztb", "ztv", T.ztb[:, 96:128:2], T.ab[:, 0:16], u, 16.0, OP.max, OP.is_lt)
+    quant("qz", 0, 128, "ztb", "ztv ztb", "qz", at=96)
+    mm(1, "qtri", 0, "qz", 128, "qtri qz")
+    tt("msk num0 num1 num2 num3 att", "bt", T.att[:, 512:576:2], T.msk[:], T.num[:], OP.mult)
+    op("V", "ps1", "o1", V.tensor_reduce, o1, T.ps1[:, 0:8], X, OP.max)
+    ts("pm1 o1 att", "at0", T.att[:, 0:512:2], T.pm1[:], o1, None, OP.is_equal)
+    quant("qab", 0, 144, "att", "att at0 bt", "qab")
+    mm(2, "qab", 0, "qab", 128, "qab", xv=16)
+
+    ts("ps2 hp", "lst", T.lst[:], T.ps2[:, 120:128], T.pc[:, 3:4], None, OP.mult)
+    cp("ps2", "off", T.off[:], T.ps2[:, 112:120])
     to_each("lst", lambda c: T.lst[:, c:c + 1], T.landL[:, 4 * r:4 * r + 1], "l2", "o2a")
     pick("snd", 0, 128, "qx", 128, "off", 0, 8, "qx off", "snd")
-    to_each("snd", lambda c: T.snd[:, CAPP * c:CAPP * c + CAPP].bitcast(dt.uint8),
-            T.slots[:, CAPP * r:CAPP * r + CAPP].bitcast(dt.uint8), "c2r", "o2b")
-    to_each("snds", lambda c: T.snds[:, CAPP * c:CAPP * c + CAPP], T.slotss[:, CAPP * r:CAPP * r + CAPP], "c2r", "o2b")
+    half = CAPP * N // 2
+    to_two("snd", [T.snd[:, half:].bitcast(dt.uint8), T.snd[:, 0:half].bitcast(dt.uint8)], T.rl[:].bitcast(dt.uint8),
+           "rc", "o2b", (0, 1))
+    to_two("snds", [T.snds[:, half:], T.snds[:, 0:half]], T.rms[:], "rp", "o2c", (2, 3))
     arrive("l2", N - 1, "landL")
-    arrive("c2r", 2 * (N - 1), "slots")
+    arrive("c2r", 4 * (N - 1), "slots")
     pick("slots", CAPP * r, CAPP * r + CAPP, "qx", 128, "off", 0, 1, "qx off", "slown")
     act("lst", "lown", T.landL[:, 4 * r:4 * r + 1], T.lst[:, 0:1], AF.Copy)
 
-    ts("o1", "st2", st2, o1, CAPP + 0.5, None, OP.is_lt)
-    ts("q2", "q32", q32, q2, 16.0, 112.0, OP.mult, OP.add)
-    ts("o1 st2", "st", st, o1, 0.5, st2, OP.is_gt, OP.mult)
-    ts("q2 best", "gn", gn, q2, 48.0, best, OP.mult, OP.add)
-    ts("o1 st", "pl", pl, o1, -1.0, st, OP.add, OP.mult)
-    ts("q32 st", "ph", ph, q32, 16.0 * (r % 2) - 256.0, st, OP.add, OP.mult)
-    ts("gn", "gn", gn, gn, 337.0, None, OP.add)
-    ts("ph", "ph", ph, ph, 256.0, None, OP.add)
-    for k, (c, n, m, sc, rd) in enumerate(((64, 8, "m8", lo, "lo"), (65, 8, "m8", hi, "hi"), (66, 8, "m8", q32, "q32"),
-                                           (0, 16, "m16", pl, "pl"), (1, 16, "m16", ph, "ph"))):
-        act(m + " b2t " + rd, "w%d" % k, T.b2t[:, c:c // 32 * 32 + 4 * n:4], T[m][:], AF.Copy, scale=sc)
-    quant("qe", 0, 512, "et", "et0 et1 et2 et3 e0 e1 e2 e3", "qe")
     for b in range(4):
-        mm(4 + b, "qe", 128 * b, "qx", 128, "qe qx")
-        act("ps%d" % (4 + b), "dan%d" % b, T.dan[:, 32 * b:32 * b + 32], T["ps%d" % (4 + b)][:, 0:A], AF.Copy)
-    quant("qb2", 0, 128, "b2t", "b2t w0 w1 w2 w3 w4", "qb2")
-    mm(3, "qa2", 0, "qb2", 128, "qa2 qb2")
+        quant("qe", 128 * b, 128, "et", "et e", "qe%d" % b, at=4 - b)
+        mm(4 + b, "qe", 128 * b, "qn", 128, "qe%d qn" % b, stop=False)
+    fill("", "aw", T.aw[:], 0.0)
+    fill("", "mz", T.mz[:, 4 * A:512], 0.0)
     quant("qw", 0, 512, "wt", "wt", "qw")
+    ts("row8 ph16", "m8", T.m8[:], T.row8[:], T.pf[:, 1:2], None, OP.is_equal)
+    ts("row16 ph16", "m16", T.m16[:], T.row16[:], T.pf[:, 1:2], None, OP.is_equal)
+    fill("", "ct2", T.ct2[:], 0.0)
 
     for c in range(4):
         la, lb = T.landL[:, 8 * c:8 * c + 1], T.landL[:, 8 * c + 4:8 * c + 5]
         if c < 2:
-            ts("landL lown zz0", "lx%d" % c, T.lx[:, 32 * c:32 * c + 32], T.zz[:, 0:32], la, lb, OP.add, OP.add)
+            ts("landL lown zz", "lx%d" % c, T.lx[:, 32 * c:32 * c + 32], T.zz[:, 0:32], la, lb, OP.add, OP.add)
         else:
             act("landL lown ones", "lx%d" % c, T.lx[:, 32 * c:32 * c + 32], T.ones[:, 0:32], AF.Identity, bias=lb, scale=la)
     op("V", "lx0 lx1 lx2 lx3", "arow", V.transpose, T.arow[:], T.lx[:])
-    ts("arow a0", "eq0", T.eq[:, 0:128], T.arow[:], T.pc[:, 1:2], None, OP.is_equal)
-    ts("arow a1c", "eq1", T.eq[:, 128:256], T.arow[:], T.pc[:, 2:3], None, OP.is_equal)
-    op("V", "rs eq0 eq1", "cc", V.tensor_tensor_scan, T.cc[:], T.rs[:], T.eq[:], 0.0, OP.mult, OP.add)
+    H = [slice(0, 128), slice(128, 256)]
     for h in range(2):
-        act("cc", "F%d j%d" % (h, h), T.j12[:, 128 * h:128 * h + 128], T.cc[:, 128 * h:128 * h + 128], AF.Relu, bias=1.0,
-            scale=-1.0, accum_out=T.F4[:, h:h + 1])
-    ts("cc", "c2", T.c2[:], T.cc[:], 1.5, None, OP.is_lt)
+        ts("arow a0 a1c", "eq%d" % h, T.eq[:, H[h]], T.arow[:], T.pc[:, 1 + h:2 + h], None, OP.is_equal)
     for h in range(2):
-        op("V", "c2", "F%d" % (2 + h), V.tensor_reduce, T.F4[:, 2 + h:3 + h], T.c2[:, 128 * h:128 * h + 128], X, OP.add)
-    cp("F0 F1 F2 F3", "fs", T.fs[:], T.F4[:])
+        op("V", "ones eq%d" % h, "cc%d" % h, V.tensor_tensor_scan, T.cc[:, H[h]], T.ones[:], T.eq[:, H[h]], 0.0, OP.mult, OP.add)
+        act("cc%d" % h, "F%d j%d" % (h, h), T.j12[:, H[h]], T.cc[:, H[h]], AF.Relu, bias=1.0, scale=-1.0,
+            accum_out=T.F4[:, h:h + 1])
+    for h in range(2):
+        ts("cc%d" % h, "c2%d" % h, T.c2[:, H[h]], T.cc[:, H[h]], 1.5, None, OP.is_lt)
+    for h in range(2):
+        op("V", "c2%d" % h, "F%d" % (2 + h), V.tensor_reduce, T.F4[:, 2 + h:3 + h], T.c2[:, H[h]], X, OP.add)
     ts("F0 F1 F2 F3", "n1", T.n1[:], T.F4[:], 127.5, None, OP.is_gt)
+    cp("F0 F1 F2 F3", "fs", T.fs[:], T.F4[:])
     tt("n1 jw", "n2", T.n2[:], T.n1[:], T.jw[:, 0:4], OP.mult)
     tt("n2 F0 F1 F2 F3", "n3", T.n3[:], T.n2[:], T.F4[:], OP.add)
     cp("n3", "sof", T.sof[:], T.n3[:])
@@ -333,62 +373,77 @@ def rank_program(g, core, T, topo):
 
     pick("pk", 0, 64, "slots", 256, "fs", 0, 4, "slots slown slowns slz fs", "pk")
     for b in range(4):
-        mm(4 + b, "qe", 128 * b, "pk", 128, "qe pk pks pkz")
-    ts("F0 F1", "jf0", T.jf[:, 0:2], T.F4[:, 0:2], 127.5, 128.0 + A * r, OP.is_lt, OP.mult)
-    cp("jw", "jf2", T.jf[:, 2:8], T.jw[:, 2:8])
-    tt("jf0 jw", "jf1", T.jf[:, 0:2], T.jf[:, 0:2], T.jw[:, 0:2], OP.add)
-    for k in range(5):
-        if k < 4:
-            tt("ps%d dan%d" % (4 + k, k), "tb%d" % k, T.tb[:, 32 * k:32 * k + 32], T["ps%d" % (4 + k)][:, 0:A],
-               T.dan[:, 32 * k:32 * k + 32], OP.add)
-        if k:
-            b = k - 1
-            tt("ps%d tb%d mt" % (4 + b, b), "mt%d" % b, T.mt[:, b:4 * A:4], T["ps%d" % (4 + b)][:, A:2 * A],
-               T.tb[:, 32 * b:32 * b + 32], OP.add)
-    quant("km", 0, 128, "mt", "mt mt0 mt1 mt2 mt3", "km")
-    cp("ps3", "posD", T.posD[:], T.ps3[:, 0:16])
-    tt("ps3 jn", "tmp", T.tmp[:], T.ps3[:, 16:24], T.jn[:], OP.add)
+        mm(4 + b, "qe", 128 * b, "pk", 128, "qe%d pk pks pkz" % b, start=False)
+    ts("o1", "st2", st2, o1, 64.0 + CAPP + 0.5, None, OP.is_lt)
+    ts("q2", "q32", q32, q2, 16.0, -16.0, OP.mult, OP.add)
+    ts("q2 best", "gn", gn, q2, 48.0, best, OP.mult, OP.add)
+    ts("o1 st2", "st", st, o1, 64.5, st2, OP.is_gt, OP.mult)
+    for b in range(4):
+        src, tb = T["ps%d" % (4 + b)], T.tb[:, 32 * b:32 * b + 32]
+        if b < 3:
+            act("ps%d" % (4 + b), "tb%d" % b, tb, src[:, A:2 * A], AF.Copy)
+        else:
+            cp("ps%d" % (4 + b), "tb%d" % b, tb, src[:, A:2 * A])
+        tt("ps%d tb%d" % (4 + b, b), "mt%d" % b, T.mz[:, b:4 * A:4], src[:, 0:A], tb, OP.add)
+    quant("km", 0, 128, "mz", "mz mt0 mt1 mt2 mt3", "km")
+    ts("o1 st", "pl", pl, o1, -65.0, st, OP.add, OP.mult)
+    ts("q32 st", "ph", ph, q32, 16.0 * (r % 2) - 256.0, st, OP.add, OP.mult)
+    ts("gn", "gn", gn, gn, -47.0, None, OP.add)
     for i in range(4):
         mm(i, "qw", 128 * i, "km", 128, "qw km")
-        layer(i, "ht", A, "ht%d" % i, "ht", True)
-    quant("hq", 0, 128, "ht", "ht ht0 ht1 ht2 ht3", "hq")
+        layer(i, "mz", 512, A, "ht%d" % i, True)
+    quant("hq", 0, 128, "mz", "mz ht0 ht1 ht2 ht3", "hq", at=128)
 
-    to_all("hq", T.hq[:, 0:A].bitcast(dt.uint8), T.hw[:, 128 + A * r:128 + A * r + A].bitcast(dt.uint8), "h3", "o3b")
-    to_all("hq", T.hqs[:, 0:A], T.hws[:, 128 + A * r:128 + A * r + A], "h3", "o3b")
+    n0 = 128 - A
+    to_two("hq", [T.hqs[:, n0:128]] * 2, T.rhs[:], "rk", "o3c", (2, 3))
+    to_all("hq", T.hq[:, n0:128].bitcast(dt.uint8), T.hw[:, 128 + A * r:128 + A * r + A].bitcast(dt.uint8), "h3", "o3b")
     arrive("m3", width * (N - 1), "land3")
     arrive("h3", 2 * width * (N - 1), "hwr")
+    ts("ph", "ph", ph, ph, 256.0, None, OP.add)
+    ts("pm1 a65 ct2", "ca", T.ct2[:, 0:512:2], T.pm1[:], T.pc[:, 4:5], None, OP.is_equal)
+    for k, (c, n, m, sc, rd) in enumerate(((64, 8, "m8", d16, "d16"), (66, 8, "m8", q32, "q32"),
+                                           (0, 16, "m16", pl, "pl"), (2, 16, "m16", ph, "ph"))):
+        act(m + " ztb " + rd, "w%d" % k, T.ztb[:, c:c // 32 * 32 + 4 * n:4], T[m][:], AF.Copy, scale=sc)
+    quant("qa2", 0, 128, "ct2", "ct2 ca", "qa2")
     cp("at", "adown", T.land3[:, 8 * r:8 * r + 4], T.at[:, 0:128:32])
-    pick("hw", 128 + A * r, 128 + A * r + A, "hq", 128, "il", 0, 2, "hq il0 il1", "hwn")
-    quant("qv", 0, 128, "vt", "vt", "qv")
-    fill("", "ar0", T.ar[:, 256:272], 0.0)
-    for i in range(4):
-        mm(i, "qw", 128 * i, "qx", 128, "qw qx")
-        layer(i, "hot", 128, "ho%d" % i, "", False)
-    quant("hw", 0, 128, "hot", "ho0 ho1 ho2 ho3", "hwo")
+    ts("F0 F1", "jf0", T.jf[:, 0:2], T.F4[:, 0:2], 127.5, 128.0 + A * r, OP.is_lt, OP.mult)
+    pick("hw", 128 + A * r, 128 + A * r + A, "hq", 128, "il", 0, 2, "hq il0 il1", "hwn", at=n0)
+    quant("qb2", 0, 128, "ztb", "ztb ztv w0 w1 w2 w3", "qb2")
+    mm(7, "qa2", 0, "qb2", 128, "qa2 qb2")
     for q in range(N):
         col = T.land3[:, 8 * q + r // 2:8 * q + r // 2 + 1]
         if q % 2:
             ts("land3 adown ones", "ax%d" % q, T.ax[:, 32 * q:32 * q + 32], T.ones[:, 0:32], 0.0, col, OP.mult, OP.add)
         else:
-            act("land3 adown zz0", "ax%d" % q, T.ax[:, 32 * q:32 * q + 32], T.zz[:, 0:32], AF.Identity, bias=col)
+            act("land3 adown zz", "ax%d" % q, T.ax[:, 32 * q:32 * q + 32], T.zz[:, 0:32], AF.Identity, bias=col)
+    for i in range(4):
+        mm(i, "qw", 128 * i, "qx", 128, "qw qx")
+        layer(i, "hot", 0, 128, "ho%d" % i, False)
+    cp("ps7", "posD", T.posD[:], T.ps7[:, 0:16])
     op("V", " ".join("ax%d" % q for q in range(N)), "ar", V.transpose, T.ar[:, 0:256], T.ax[:])
+    fill("", "ar0", T.ar[:, 256:272], 0.0)
+    tt("ps7 jn", "tmp", T.tmp[:], T.ps7[:, 16:24], T.jn[:], OP.add)
     cp("ar ar0 posD", "aj", T.aj[:], T.ar[:, 0:272].indirect(T.posD[:, 0:16]))
+    cp("jw", "jf2", T.jf[:, 2:8], T.jw[:, 2:8])
     op("V", "aj", "ajt", V.transpose, T.ajt[:], T.aj[:])
+    tt("jf0 jw", "jf1", T.jf[:, 0:2], T.jf[:, 0:2], T.jw[:, 0:2], OP.add)
     tt("ajt tmp", "f1", T.f1[:], T.ajt[:, 0:256:32], T.tmp[:], OP.mult)
     tt("f1 jf1 jf2", "f2", T.f2[:], T.f1[:], T.jf[:], OP.add)
     cp("f2", "fin", T.fin[:], T.f2[:])
-    tt("ajt m8", "mw2", T.mw2[:], T.ajt[:, 0:256:32], T.m8[:], OP.mult)
-    op("V", "mw2", "mn", V.tensor_reduce, mn, T.mw2[:], X, OP.add)
-    ts("mn gn", "mgc", mgc, mn, gn, -1.0, OP.mult, OP.add)
-    dma("S", "mgc", "mgo", T.mg[:], mgc)
+    quant("hw", 0, 128, "hot", "ho0 ho1 ho2 ho3", "hwo")
+    quant("qv", 0, 128, "vt", "vt", "qv")
 
     pick("fo", 0, 128, "hw", 384, "fin", 0, 8, "hwo hwr hwn hwns fin", "fo")
     mm(4, "qv", 0, "fo", 128, "qv fo fos")
     dma("S", "fo", "oco", T.oc[:], T.fo[:].bitcast(dt.uint8))
     for k in range(4):
         dma("A", "fos", "osco%d" % k, T.osc[4 * k:4 * k + 4, :], T.fos[32 * k:32 * k + 4, :])
+    tt("ajt m8", "mw2", T.mw2[:], T.ajt[:, 0:256:32], T.m8[:], OP.mult)
+    op("V", "mw2", "mn", V.tensor_reduce, mn, T.mw2[:], X, OP.add)
     cp("ps4", "yo", T.yo[:], T.ps4[:, 0:128])
     dma("S", "yo", "yout", T.y[:], T.yo[:])
+    ts("mn gn", "mgc", mgc, mn, gn, -1.0, OP.mult, OP.add)
+    dma("S", "mgc", "mgo", T.mg[:], mgc)
     for s, v in count.items():
         if known["S"].get(s, 0) < v:
             SY.wait_ge(S[s], v)

from concourse.bass import DstId, RemoteDMATransfer
from concourse.mybir import dt, AluOpType, AxisListType, ActivationFunctionType

F32, BF, U16, I32, MXC, U8 = "float32", "bfloat16", "uint16", "int32", "float8_e4m3fn_x4", "uint8"
SCRATCH = {}


def _buf(name, cols, dtype):
    SCRATCH[name] = ("sbuf", [128, cols], dtype)


def _mx(name, cols):
    _buf(name, cols, MXC)
    _buf(name + "s", cols, U8)


for _n, _c in (("qx", 128), ("qn", 128), ("anc", 288), ("qtri", 128), ("qa2", 128), ("qe", 512), ("qz", 128), ("qab", 144),
               ("qb2", 128), ("snd", 128), ("slots", 256), ("pk", 192), ("qw", 512), ("qv", 128), ("km", 128),
               ("hq", 128), ("hw", 384), ("fo", 128)):
    _mx(_n, _c)
_buf("rl", 64, MXC)
_buf("rms", 64, U8)
_buf("rhs", 32, U8)
for _n, _c in (("xt", 512), ("xa", 512), ("wt", 2048), ("vt", 512), ("ct", 512), ("ct2", 512), ("et", 516), ("ztb", 608),
               ("att", 576), ("zz", 512), ("mz", 640), ("hot", 512), ("ones", 128), ("ident", 128),
               ("tri", 128), ("pm1", 256), ("lx", 128), ("arow", 128), ("eq", 256), ("cc", 256), ("c2", 256),
               ("j12", 256), ("aw", 192), ("at", 128), ("adm4", 8), ("land3", 64), ("ax", 256), ("ar", 272), ("aj", 256),
               ("ajt", 256)):
    _buf(_n, _c, BF)
for _n, _c in (("R", 288), ("mrow", 32), ("thr", 64), ("t1", 64), ("t2", 97), ("sc", 16), ("jr", 256),
               ("j7", 16), ("ab", 32), ("pen", 32), ("msk", 32), ("num", 32), ("qi", 8), ("qc", 32), ("ri", 16), ("qh", 16),
               ("crow", 32), ("row8", 8), ("row16", 16), ("pf", 4), ("pc", 8), ("m8", 8), ("m16", 16), ("jw", 8), ("jn", 8),
               ("lst", 8), ("landL", 32), ("F4", 4), ("tb", 128), ("n1", 4), ("n2", 4), ("n3", 4), ("tmp", 8),
               ("jf", 8), ("f1", 8), ("f2", 8), ("mw2", 8), ("yo", 128)):
    _buf(_n, _c, F32)
for _n, _c in (("il", 2), ("off", 8), ("fs", 4), ("sof", 4), ("posD", 16), ("fin", 8)):
    _buf(_n, _c, U16)
_buf("pi", 1, I32)
_buf("pin", 4, I32)
for _i in range(8):
    SCRATCH["ps%d" % _i] = ("psum", [128, 512], F32)
SEMAPHORES = (["cV", "cA", "cP", "cG", "a1", "o1s", "l2", "c2r", "o2a", "o2b", "o2c", "m3", "o3a", "h3", "o3b", "o3c",
               "rc", "rp", "rk", "hl"] + ["d%d" % _i for _i in range(12)])


def to(topo, c):
    return DstId(rid=topo.addr(c)[0], pnc=topo.addr(c)[1])


def plan(own, r, T, topo):
    for b in ((2, 1, 0), (0, 2, 1), (1, 2, 0)):
        order = [r ^ sum((c >> (2 - i) & 1) << b[i] for i in range(3)) for c in range(8)]
        if all(topo.same_plane(topo.chip(own), topo.chip(T.cores[q])) for q in order[1:4]):
            break
    near, far = [T.cores[q] for q in order[1:4]], [T.cores[q] for q in order[4:]]
    rest = sorted([c for c in topo.cores_of(own) if c != own], key=lambda c: topo.die(c) == topo.die(own))
    f = [c for c in rest if all(topo.may_write(c, d) for d in far)][:2]
    n = [c for c in rest if c not in f and all(topo.may_write(c, d) for d in near)][:2]
    return order, near, far, [f[0], n[0], f[1], n[1]]


def hand_on(g, core, r, role, near, far, T, topo):
    S, CAPP, A = T.sem, 16, 32
    goal, first = (near, 1) if role % 2 else (far, 0)
    eng = topo.engines(core, goal[0])

    def piece(i):
        a = CAPP * (i + first)
        return T.rms[:, a:a + CAPP] if role >= 2 else T.rl[:, a:a + CAPP].bitcast(dt.uint8)

    land = T.slotss[:, CAPP * r:CAPP * r + CAPP] if role >= 2 else T.slots[:, CAPP * r:CAPP * r + CAPP].bitcast(dt.uint8)
    g.wait_ge(S.rp if role >= 2 else S.rc, 4)
    g.remote_dma_fused([RemoteDMATransfer(dst_ids=[to(topo, d)], dma_engine_mask=1 << eng[2 * i] | 1 << eng[2 * i + 1],
                                          remote_sem=S.c2r, src=piece(i), dst=land) for i, d in enumerate(goal)], local_sem=S.hl)
    n = 2 * len(goal)
    if role >= 2:
        g.wait_ge(S.rk, 4)
        g.remote_dma_fused([RemoteDMATransfer(dst_ids=[to(topo, d) for d in goal], dma_engine_mask=topo.mask(core, goal[0]),
                                              remote_sem=S.h3, srcs=[T.rhs[:, 0:A]],
                                              dsts=[T.hws[:, 128 + A * r:128 + A * r + A]] * len(goal))], local_sem=S.hl)
        n += len(eng)
    g.wait_ge(S.hl, n)


def rank_program(g, core, T, topo):
    N, S = len(T.cores), T.sem
    A, CAPP, KM = 32, 16, 48
    mine = [c for c in T.cores if topo.chip(c) == topo.chip(core)]
    if not mine:
        return
    r = T.rank_of(mine[0])
    order, near, far, help4 = plan(mine[0], r, T, topo)
    if core != mine[0]:
        if core in help4:
            hand_on(g, core, r, help4.index(core), near, far, T, topo)
        return
    OP, AF, X = AluOpType, ActivationFunctionType, AxisListType.X
    V, AC, PE, SY = g.vector, g.scalar, g.tensor, g.sync
    tiny = 1e-29

    qs = {"V": V, "A": AC, "P": PE, "G": g, "S": SY}
    count, known = {}, {q: {} for q in qs}
    writer, readers = {}, {}

    def before(q, rd, wr):
        need = [writer[k] for k in rd if k in writer]
        for k in list(wr) + [k for k in rd if k.startswith("ps")]:
            if k in writer:
                need.append(writer[k])
            need += readers.get(k, [])
        best = {}
        for s, v, clk in need:
            if known[q].get(s, 0) < v and best.get(s, (0,))[0] < v:
                best[s] = (v, clk)
        for s in list(best):
            if not any(o != s and best[o][1].get(s, 0) >= best[s][0] for o in best):
                qs[q].wait_ge(S[s], best[s][0])
        for s, (v, clk) in best.items():
            known[q][s] = max(known[q].get(s, 0), v)
            for a, b in clk.items():
                known[q][a] = max(known[q].get(a, 0), b)

    def after(tok, rd, wr):
        for k in wr:
            writer[k] = tok
            readers[k] = []
        for k in rd:
            readers.setdefault(k, []).append(tok)

    def op(q, rd, wr, fn, *args, **kw):
        rd, wr = rd.split(), wr.split()
        before(q, rd, wr)
        s = "c" + q
        count[s] = count.get(s, 0) + 1
        fn(*args, **kw).then_inc(S[s], 1)
        after((s, count[s], dict(known[q])), rd, wr)

    dn = [0]

    def dma(q, rd, wr, out, in_):
        rd, wr = rd.split(), wr.split()
        before(q, rd, wr)
        s = "d%d" % dn[0]
        dn[0] += 1
        count[s] = 16
        qs[q].dma_start(out, in_).then_inc(S[s], 16)
        after((s, 16, dict(known[q])), rd, wr)

    def arrive(s, n, wr):
        count[s] = n
        after((s, n, {}), [], wr.split())

    others = [T.cores[q] for q in order[1:]]
    allm = topo.mask(core, others[0])
    for c in others:
        allm &= topo.mask(core, c)
    eng = [e for e in topo.engines(core, others[0]) if allm >> e & 1]
    width = len(eng)
    side = [e for e in topo.engines(core, help4[0]) if e not in eng]

    def to_all(rd, src, dstap, sem, loc):
        before("G", rd.split(), [])
        g.remote_dma_fused([RemoteDMATransfer(dst_ids=[to(topo, c) for c in others], dma_engine_mask=allm, remote_sem=S[sem],
                                              srcs=[src], dsts=[dstap] * len(others))], local_sem=S[loc])
        count[loc] = count.get(loc, 0) + width

    def to_each(rd, src, dstap, sem, loc):
        before("G", rd.split(), [])
        g.remote_dma_fused([RemoteDMATransfer(dst_ids=[to(topo, others[c - 1])], dma_engine_mask=1 << eng[c - 1],
                                              remote_sem=S[sem], src=src(c), dst=dstap) for c in range(1, N)],
                           local_sem=S[loc])
        count[loc] = count.get(loc, 0) + N - 1

    def to_two(rd, src, dstap, sem, loc, roles):
        before("G", rd.split(), [])
        h = len(side) // 2
        g.remote_dma_fused([RemoteDMATransfer(dst_ids=[to(topo, help4[k])],
                                              dma_engine_mask=sum(1 << e for e in side[h * i:h * i + h]),
                                              remote_sem=S[sem], src=src[i], dst=dstap) for i, k in enumerate(roles)],
                           local_sem=S[loc])
        count[loc] = count.get(loc, 0) + 2 * h

    def ts(rd, wr, out, in0, s1, s2, *ops):
        op("V", rd, wr, V.tensor_scalar, out, in0, s1, s2, *ops)

    def tt(rd, wr, out, in0, in1, o):
        op("V", rd, wr, V.tensor_tensor, out, in0, in1, o)

    def cp(rd, wr, out, in_):
        op("V", rd, wr, V.tensor_copy, out, in_)

    def fill(rd, wr, out, c):
        op("V", rd, wr, V.memset, out, c)

    def act(rd, wr, out, in_, f, **kw):
        op("A", rd, wr, AC.activation, out, in_, f, **kw)

    def iota(wr, out, pattern, base=0, mult=0):
        op("G", "", wr, g.iota, out, pattern, base, mult, allow_small_or_imprecise_dtypes=True)

    def mm(bank, w, wv, x, n, rd, xv=0, start=True, stop=True):
        op("P", rd, "ps%d" % bank, PE.matmul_mx, T["ps%d" % bank][:, 0:n], T[w][:, wv:wv + 128], T[w + "s"][:, wv:wv + 128],
           T[x][:, xv:xv + n], T[x + "s"][:, xv:xv + n], start, stop)

    def quant(out, a, n, tile, rd, wr, at=0):
        op("V", rd, wr, V.quantize_mx, T[out][:, a:a + n], T[out + "s"][:, a:a + n], T[tile][:, at:at + 4 * n])

    def pick(out, a, b, win, w, lists, la, lb, rd, wr, at=0):
        cp(rd, wr, T[out][:, a:b].bitcast(dt.uint32), T[win][:, at:w].bitcast(dt.uint32).indirect(T[lists][:, la:lb]))
        act(rd, wr + "s", T[out + "s"][:, a:b], T[win + "s"][:, at:w].indirect(T[lists][:, la:lb]), AF.Copy)

    def layer(i, tile, a, n, wr, both):
        src, out = T["ps%d" % i][:, 0:n], T[tile][:, a + i:a + 4 * n:4]
        if i % 2 and both:
            ts("ps%d" % i, wr, out, src, 0.0, 0.0625, OP.max, OP.mult)
        else:
            act("ps%d" % i, wr, out, src, AF.Relu, scale=0.0625)

    dma("S", "", "xa", T.xa[:, 0:4 * A], T.x[:, 0:4 * A])
    dma("S", "", "xt", T.xt[:], T.x[:])
    op("G", "", "pi", g.iota, T.pi[:], [[0, 1]], 0, 1)
    iota("qi", T.qi[:], [[A * (order[c] - r), 2] for c in (4, 2, 1)], A * r)
    fill("", "ones", T.ones[:], 1.0)
    op("G", "ones", "tri", g.affine_select, T.tri[:], T.ones[:], [[1, 128]], OP.is_ge, 0.0, 0, -1)
    fill("", "xaz", T.xa[:, 4 * A:], 0.0)
    fill("", "zz", T.zz[:], 0.0)
    ts("pi", "pin", T.pin[:, 0:1], T.pi[:], 15, None, OP.bitwise_and)
    quant("qn", 0, 128, "xa", "xa xaz", "qn")

    to_all("qn", T.qn[:, 0:A].bitcast(dt.uint8), T.anc[:, A * r:A * r + A].bitcast(dt.uint8), "a1", "o1s")
    to_all("qn", T.qns[:, 0:A], T.ancs[:, A * r:A * r + A], "a1", "o1s")
    arrive("a1", 2 * width * (N - 1), "anc")
    SY.wait_ge(S.o1s, 2 * width)
    known["S"]["o1s"] = 2 * width
    dma("S", "", "wt", T.wt[:], T.w[:])
    dma("S", "", "vt", T.vt[:], T.v[:])

    op("G", "ones", "ident", g.affine_select, T.ident[:], T.ones[:], [[1, 128]], OP.is_equal, 0.0, 0, -1)
    iota("ri", T.ri[:, 0:15], [[A, 15]], -7 * A)
    iota("crow", T.crow[:], [[1, 32]])
    iota("pm1", T.pm1[:], [[0, 8], [1, 16], [0, 2]], 65)
    iota("row8", T.row8[:], [[1, 8]])
    iota("row16", T.row16[:], [[1, 8], [0, 2]])
    for k in range(4):
        act("qi", "qc%d" % k, T.qc[:, k // 2 * 16 + k % 2:k // 2 * 16 + 16:2], T.qi[:], AF.Identity, bias=0.5 * A - 0.5)
    act("zz", "num3", T.num[:, 17:32:2], T.zz[:, 0:8], AF.Identity, bias=32.0)
    ts("pin", "il0", T.il[:, 0:1], T.pin[:, 0:1], 0, None, OP.add)
    ts("pin", "il1", T.il[:, 1:2], T.pin[:, 0:1], 16, None, OP.add)
    fill("", "ct", T.ct[:], 0.0)
    for a, k in ((A * r, "own"), (N * A, "pad")):
        pick("anc", a, a + A, "qn", 128, "il", 0, 2, "qn il0 il1", "anc" + k)
    ts("pi", "pin1", T.pin[:, 1:2], T.pi[:], 4, None, OP.arith_shift_right)
    ts("pi", "pin2", T.pin[:, 2:3], T.pi[:], 31, None, OP.bitwise_and)
    cp("pin", "pm", T.pf[:, 0:1], T.pin[:, 0:1])
    cp("pin1", "ph16", T.pf[:, 1:2], T.pin[:, 1:2])
    cp("pin2", "p31", T.pf[:, 2:3], T.pin[:, 2:3])
    act("tri ct", "ctri", T.ct[:, 0:512:4], T.tri[:], AF.Copy)
    act("ident ct", "cid", T.ct[:, 2:512:4], T.ident[:], AF.Copy, scale=64.0)
    act("zz pm", "num0", T.num[:, 0:16:2], T.zz[:, 0:8], AF.Identity, bias=T.pf[:, 0:1])
    act("ph16", "khi", T.pc[:, 0:1], T.pf[:, 1:2], AF.Copy, scale=16.0)
    quant("qx", 0, 128, "xt", "xt", "qx")
    act("zz khi", "num1", T.num[:, 1:16:2], T.zz[:, 0:8], AF.Identity, bias=T.pc[:, 0:1])
    act("pm", "a0", T.pc[:, 1:2], T.pf[:, 0:1], AF.Identity, bias=16.0)
    act("pm", "a1c", T.pc[:, 2:3], T.pf[:, 0:1], AF.Identity, bias=32.0)
    act("pm", "a65", T.pc[:, 4:5], T.pf[:, 0:1], AF.Identity, bias=65.0)
    ts("crow p31", "thr0", T.thr[:, 0:32], T.crow[:], T.pf[:, 2:3], tiny, OP.is_lt, OP.mult)
    fill("", "thr1", T.thr[:, 32:64], 0.0)
    fill("", "kk", T.t2[:, 96:97], 16.0 - KM + 0.5)
    fill("", "t10", T.t1[0:32, 32:64], 0.0)
    fill("", "t20", T.t2[0:32, 64:96], 0.0)
    fill("thr1", "thr2", T.thr[96:128, 32:64], tiny)
    fill("kk", "kk", T.t2[0:32, 96:97], 1000.0)
    ts("ri", "qh", T.qh[:, 0:15], T.ri[:, 0:15], -0.5, None, OP.add)
    quant("qtri", 0, 128, "ct", "ctri cid ct", "qtri")
    fill("", "ztb", T.ztb[:], 0.0)
    fill("", "att", T.att[:], 0.0)
    ts("p31", "hp", T.pc[:, 3:4], T.pf[:, 2:3], 15.5, float(r % 2), OP.is_gt, OP.is_equal)

    fill("", "et", T.et[:], 0.0)
    act("ident et", "e", T.et[:, 4:516:4], T.ident[:], AF.Copy, scale=0.5)
    act("row8 pm", "jw", T.jw[:], T.row8[:], AF.Identity, scale=16.0, bias=T.pf[:, 0:1])
    act("jw", "jn", T.jn[:], T.jw[:], AF.Identity, scale=-1.0, bias=144.0)
    quant("slots", 128, 128, "zz", "zz", "slz")
    quant("pk", 64, 128, "zz", "zz", "pkz")

    best, q2, d16, u, o1, st2, st, pl, ph, q32, gn, mn, mgc = [T.sc[:, i:i + 1] for i in range(13)]
    M = T.R[:, 255:256]
    mm(0, "qx", 0, "anc", 128, "qx anc ancown ancowns ancpad ancpads")
    mm(1, "qx", 0, "anc", 160, "qx anc ancown ancowns ancpad ancpads", xv=128)
    op("V", "ps0 zz", "R0", V.tensor_tensor_scan, T.R[:, 0:128], T.ps0[:, 0:128], T.zz[:, 0:128], -9.0e29, OP.max, OP.add)
    op("V", "ps1 zz R0", "R", V.tensor_tensor_scan, T.R[:, 128:288], T.ps1[:, 0:160], T.zz[:, 0:160], T.R[:, 127:128],
       OP.max, OP.add)
    op("V", "R", "m0", V.transpose, T.mrow[:], T.R[:, 256:288])

    def quad(t, q, c):
        return T[t][32 * q:32 * q + 32, c:c + 32]

    ts("R m0", "t1a", T.t1[:, 0:32], T.mrow[:], M, -1.0, OP.subtract, OP.mult)
    for a in range(1, 4):
        Ma = T.R[32 * a:32 * a + 32, 255:256]
        b = a % 3 + 1
        act("R m0", "t1%d" % a, quad("t1", a, 32), quad("mrow", b, 0), AF.Identity, scale=-1.0, bias=Ma)
        b = (a + 1) % 3 + 1
        ts("R m0", "t2%d" % a, quad("t2", a, 64), quad("mrow", b, 0), Ma, None, OP.is_ge if b < a else OP.is_gt)
    act("R", "best jr", T.jr[:], T.R[:, 0:256], AF.Sign, bias=M, scale=-1.0, accum_out=best)
    act("best qc0 qc1 qc2 qc3", "ab", T.ab[:], T.qc[:], AF.Abs, bias=best, scale=-1.0)
    act("best qh", "q2 j7", T.j7[:, 0:15], T.qh[:, 0:15], AF.Sign, bias=best, scale=-1.0, accum_out=q2)
    act("ab", "pen", T.pen[:], T.ab[:], AF.Relu, scale=-2.0, bias=32.0)
    act("q2 best", "d16", d16, q2, AF.Identity, bias=best, scale=-16.0)
    act("pen", "msk", T.msk[:], T.pen[:], AF.Sign)
    act("d16 zz", "num2", T.num[:, 16:32:2], T.zz[:, 0:8], AF.Identity, bias=d16)
    tt("t1a t11 t12 t13 t10 thr0 thr1 thr2", "t2", T.t2[:, 0:64], T.t1[:], T.thr[:], OP.is_lt)
    op("V", "t2 t20 t21 t22 t23 kk", "u", V.tensor_reduce, u, T.t2[:], X, OP.add)
    ts("ab u ztb", "ztv", T.ztb[:, 96:128:2], T.ab[:, 0:16], u, 16.0, OP.max, OP.is_lt)
    quant("qz", 0, 128, "ztb", "ztv ztb", "qz", at=96)
    mm(1, "qtri", 0, "qz", 128, "qtri qz")
    tt("msk num0 num1 num2 num3 att", "bt", T.att[:, 512:576:2], T.msk[:], T.num[:], OP.mult)
    op("V", "ps1", "o1", V.tensor_reduce, o1, T.ps1[:, 0:8], X, OP.max)
    ts("pm1 o1 att", "at0", T.att[:, 0:512:2], T.pm1[:], o1, None, OP.is_equal)
    quant("qab", 0, 144, "att", "att at0 bt", "qab")
    mm(2, "qab", 0, "qab", 128, "qab", xv=16)

    ts("ps2 hp", "lst", T.lst[:], T.ps2[:, 120:128], T.pc[:, 3:4], None, OP.mult)
    cp("ps2", "off", T.off[:], T.ps2[:, 112:120])
    to_each("lst", lambda c: T.lst[:, c:c + 1], T.landL[:, 4 * r:4 * r + 1], "l2", "o2a")
    pick("snd", 0, 128, "qx", 128, "off", 0, 8, "qx off", "snd")
    half = CAPP * N // 2
    to_two("snd", [T.snd[:, half:].bitcast(dt.uint8), T.snd[:, 0:half].bitcast(dt.uint8)], T.rl[:].bitcast(dt.uint8),
           "rc", "o2b", (0, 1))
    to_two("snds", [T.snds[:, half:], T.snds[:, 0:half]], T.rms[:], "rp", "o2c", (2, 3))
    arrive("l2", N - 1, "landL")
    arrive("c2r", 4 * (N - 1), "slots")
    pick("slots", CAPP * r, CAPP * r + CAPP, "qx", 128, "off", 0, 1, "qx off", "slown")
    act("lst", "lown", T.landL[:, 4 * r:4 * r + 1], T.lst[:, 0:1], AF.Copy)

    for b in range(4):
        quant("qe", 128 * b, 128, "et", "et e", "qe%d" % b, at=4 - b)
        mm(4 + b, "qe", 128 * b, "qn", 128, "qe%d qn" % b, stop=False)
    fill("", "aw", T.aw[:], 0.0)
    fill("", "mz", T.mz[:, 4 * A:512], 0.0)
    quant("qw", 0, 512, "wt", "wt", "qw")
    ts("row8 ph16", "m8", T.m8[:], T.row8[:], T.pf[:, 1:2], None, OP.is_equal)
    ts("row16 ph16", "m16", T.m16[:], T.row16[:], T.pf[:, 1:2], None, OP.is_equal)
    fill("", "ct2", T.ct2[:], 0.0)

    for c in range(4):
        la, lb = T.landL[:, 8 * c:8 * c + 1], T.landL[:, 8 * c + 4:8 * c + 5]
        if c < 2:
            ts("landL lown zz", "lx%d" % c, T.lx[:, 32 * c:32 * c + 32], T.zz[:, 0:32], la, lb, OP.add, OP.add)
        else:
            act("landL lown ones", "lx%d" % c, T.lx[:, 32 * c:32 * c + 32], T.ones[:, 0:32], AF.Identity, bias=lb, scale=la)
    op("V", "lx0 lx1 lx2 lx3", "arow", V.transpose, T.arow[:], T.lx[:])
    H = [slice(0, 128), slice(128, 256)]
    for h in range(2):
        ts("arow a0 a1c", "eq%d" % h, T.eq[:, H[h]], T.arow[:], T.pc[:, 1 + h:2 + h], None, OP.is_equal)
    for h in range(2):
        op("V", "ones eq%d" % h, "cc%d" % h, V.tensor_tensor_scan, T.cc[:, H[h]], T.ones[:], T.eq[:, H[h]], 0.0, OP.mult, OP.add)
        act("cc%d" % h, "F%d j%d" % (h, h), T.j12[:, H[h]], T.cc[:, H[h]], AF.Relu, bias=1.0, scale=-1.0,
            accum_out=T.F4[:, h:h + 1])
    for h in range(2):
        ts("cc%d" % h, "c2%d" % h, T.c2[:, H[h]], T.cc[:, H[h]], 1.5, None, OP.is_lt)
    for h in range(2):
        op("V", "c2%d" % h, "F%d" % (2 + h), V.tensor_reduce, T.F4[:, 2 + h:3 + h], T.c2[:, H[h]], X, OP.add)
    ts("F0 F1 F2 F3", "n1", T.n1[:], T.F4[:], 127.5, None, OP.is_gt)
    cp("F0 F1 F2 F3", "fs", T.fs[:], T.F4[:])
    tt("n1 jw", "n2", T.n2[:], T.n1[:], T.jw[:, 0:4], OP.mult)
    tt("n2 F0 F1 F2 F3", "n3", T.n3[:], T.n2[:], T.F4[:], OP.add)
    cp("n3", "sof", T.sof[:], T.n3[:])
    cp("sof ones aw", "aws", T.aw[:, 0:192].indirect(T.sof[:, 0:4]), T.ones[:, 0:64])
    op("V", "aws", "at", V.transpose, T.at[:], T.aw[:, 0:128])
    cp("at", "adm4", T.adm4[:, 0:4], T.at[:, 0:128:32])
    to_all("adm4", T.adm4[:, 0:4], T.land3[:, 8 * r:8 * r + 4], "m3", "o3a")

    pick("pk", 0, 64, "slots", 256, "fs", 0, 4, "slots slown slowns slz fs", "pk")
    for b in range(4):
        mm(4 + b, "qe", 128 * b, "pk", 128, "qe%d pk pks pkz" % b, start=False)
    ts("o1", "st2", st2, o1, 64.0 + CAPP + 0.5, None, OP.is_lt)
    ts("q2", "q32", q32, q2, 16.0, -16.0, OP.mult, OP.add)
    ts("q2 best", "gn", gn, q2, 48.0, best, OP.mult, OP.add)
    ts("o1 st2", "st", st, o1, 64.5, st2, OP.is_gt, OP.mult)
    for b in range(4):
        src, tb = T["ps%d" % (4 + b)], T.tb[:, 32 * b:32 * b + 32]
        if b < 3:
            act("ps%d" % (4 + b), "tb%d" % b, tb, src[:, A:2 * A], AF.Copy)
        else:
            cp("ps%d" % (4 + b), "tb%d" % b, tb, src[:, A:2 * A])
        tt("ps%d tb%d" % (4 + b, b), "mt%d" % b, T.mz[:, b:4 * A:4], src[:, 0:A], tb, OP.add)
    quant("km", 0, 128, "mz", "mz mt0 mt1 mt2 mt3", "km")
    ts("o1 st", "pl", pl, o1, -65.0, st, OP.add, OP.mult)
    ts("q32 st", "ph", ph, q32, 16.0 * (r % 2) - 256.0, st, OP.add, OP.mult)
    ts("gn", "gn", gn, gn, -47.0, None, OP.add)
    for i in range(4):
        mm(i, "qw", 128 * i, "km", 128, "qw km")
        layer(i, "mz", 512, A, "ht%d" % i, True)
    quant("hq", 0, 128, "mz", "mz ht0 ht1 ht2 ht3", "hq", at=128)

    n0 = 128 - A
    to_two("hq", [T.hqs[:, n0:128]] * 2, T.rhs[:], "rk", "o3c", (2, 3))
    to_all("hq", T.hq[:, n0:128].bitcast(dt.uint8), T.hw[:, 128 + A * r:128 + A * r + A].bitcast(dt.uint8), "h3", "o3b")
    arrive("m3", width * (N - 1), "land3")
    arrive("h3", 2 * width * (N - 1), "hwr")
    ts("ph", "ph", ph, ph, 256.0, None, OP.add)
    ts("pm1 a65 ct2", "ca", T.ct2[:, 0:512:2], T.pm1[:], T.pc[:, 4:5], None, OP.is_equal)
    for k, (c, n, m, sc, rd) in enumerate(((64, 8, "m8", d16, "d16"), (66, 8, "m8", q32, "q32"),
                                           (0, 16, "m16", pl, "pl"), (2, 16, "m16", ph, "ph"))):
        act(m + " ztb " + rd, "w%d" % k, T.ztb[:, c:c // 32 * 32 + 4 * n:4], T[m][:], AF.Copy, scale=sc)
    quant("qa2", 0, 128, "ct2", "ct2 ca", "qa2")
    cp("at", "adown", T.land3[:, 8 * r:8 * r + 4], T.at[:, 0:128:32])
    ts("F0 F1", "jf0", T.jf[:, 0:2], T.F4[:, 0:2], 127.5, 128.0 + A * r, OP.is_lt, OP.mult)
    pick("hw", 128 + A * r, 128 + A * r + A, "hq", 128, "il", 0, 2, "hq il0 il1", "hwn", at=n0)
    quant("qb2", 0, 128, "ztb", "ztb ztv w0 w1 w2 w3", "qb2")
    mm(7, "qa2", 0, "qb2", 128, "qa2 qb2")
    for q in range(N):
        col = T.land3[:, 8 * q + r // 2:8 * q + r // 2 + 1]
        if q % 2:
            ts("land3 adown ones", "ax%d" % q, T.ax[:, 32 * q:32 * q + 32], T.ones[:, 0:32], 0.0, col, OP.mult, OP.add)
        else:
            act("land3 adown zz", "ax%d" % q, T.ax[:, 32 * q:32 * q + 32], T.zz[:, 0:32], AF.Identity, bias=col)
    for i in range(4):
        mm(i, "qw", 128 * i, "qx", 128, "qw qx")
        layer(i, "hot", 0, 128, "ho%d" % i, False)
    cp("ps7", "posD", T.posD[:], T.ps7[:, 0:16])
    op("V", " ".join("ax%d" % q for q in range(N)), "ar", V.transpose, T.ar[:, 0:256], T.ax[:])
    fill("", "ar0", T.ar[:, 256:272], 0.0)
    tt("ps7 jn", "tmp", T.tmp[:], T.ps7[:, 16:24], T.jn[:], OP.add)
    cp("ar ar0 posD", "aj", T.aj[:], T.ar[:, 0:272].indirect(T.posD[:, 0:16]))
    cp("jw", "jf2", T.jf[:, 2:8], T.jw[:, 2:8])
    op("V", "aj", "ajt", V.transpose, T.ajt[:], T.aj[:])
    tt("jf0 jw", "jf1", T.jf[:, 0:2], T.jf[:, 0:2], T.jw[:, 0:2], OP.add)
    tt("ajt tmp", "f1", T.f1[:], T.ajt[:, 0:256:32], T.tmp[:], OP.mult)
    tt("f1 jf1 jf2", "f2", T.f2[:], T.f1[:], T.jf[:], OP.add)
    cp("f2", "fin", T.fin[:], T.f2[:])
    quant("hw", 0, 128, "hot", "ho0 ho1 ho2 ho3", "hwo")
    quant("qv", 0, 128, "vt", "vt", "qv")

    pick("fo", 0, 128, "hw", 384, "fin", 0, 8, "hwo hwr hwn hwns fin", "fo")
    mm(4, "qv", 0, "fo", 128, "qv fo fos")
    dma("S", "fo", "oco", T.oc[:], T.fo[:].bitcast(dt.uint8))
    for k in range(4):
        dma("A", "fos", "osco%d" % k, T.osc[4 * k:4 * k + 4, :], T.fos[32 * k:32 * k + 4, :])
    tt("ajt m8", "mw2", T.mw2[:], T.ajt[:, 0:256:32], T.m8[:], OP.mult)
    op("V", "mw2", "mn", V.tensor_reduce, mn, T.mw2[:], X, OP.add)
    cp("ps4", "yo", T.yo[:], T.ps4[:, 0:128])
    dma("S", "yo", "yout", T.y[:], T.yo[:])
    ts("mn gn", "mgc", mgc, mn, gn, -1.0, OP.mult, OP.add)
    dma("S", "mgc", "mgo", T.mg[:], mgc)
    for s, v in count.items():
        if known["S"].get(s, 0) < v:
            SY.wait_ge(S[s], v)
